import numpy as np
import ml_dtypes


def mxq(x, axis, fmt="e4m3"):
    dtype, down = {"e4m3": (ml_dtypes.float8_e4m3fn, 7), "e5m2": (ml_dtypes.float8_e5m2, 14)}[fmt]
    v = np.moveaxis(np.asarray(x, np.float32).astype(ml_dtypes.bfloat16).astype(np.float64), axis, -1)
    blocks = v.reshape(v.shape[:-1] + (-1, 32))
    amax = np.abs(blocks).max(-1, keepdims=True)
    byte = np.maximum(np.where(amax > 0, np.frexp(amax)[1] - 1 + 127, 0) - down, 1)
    scale = np.exp2(byte - 127.0)
    codes = (blocks / scale).astype(np.float32).astype(dtype).astype(np.float64)
    return np.moveaxis((codes * scale).reshape(v.shape), -1, axis)


WIDE = False


def mx_kscale(k):
    if not WIDE:
        return np.ones(k)
    levels = np.array([18, -18])
    if k % 512:
        return np.exp2(np.random.permutation(np.resize(levels, k // 32))).repeat(32)
    a = np.empty((k // 512, 16))
    for p in range(k // 512):
        a[p, :8] = np.random.permutation(np.resize(levels, 8))
        for g in range(8):
            far = levels[np.abs(levels - a[p, g]) >= 10]
            a[p, g + 8] = far[np.random.randint(len(far))]
    return np.exp2(a.ravel()).repeat(32)


def f64(x):
    return np.asarray(x).astype(np.float64)


def striped(idx):
    return np.tile(np.asarray(idx).reshape(-1, 16).T, (8, 1)).astype(np.uint16)


def unstriped(offs):
    return offs[:16].T.reshape(-1).astype(np.int64)


B, N, T, D, R = 2, 512, 2048, 512, 512


def setup_inputs():
    n = np.random.standard_normal
    idx = np.random.permutation(T)[:B * N]
    s = mx_kscale(D)[:, None]
    z = mx_kscale(R)[:, None]
    q = n((B, D, R))
    do = n((B, D, R))
    return {
        "qT": (q * s).astype(np.float32),
        "cT": (n((D, T)) * (1.00 / np.sqrt(D)) / s).astype(np.float32),
        "doT": (do * s).astype(np.float32),
        "rw": (np.random.uniform(0.5, 1.5, (B, R, 1)) * 1.0 / np.sqrt(R) * z).astype(np.float32),
        "qm": (q.transpose(0, 2, 1) / z).astype(np.float32),
        "dom": (do.transpose(0, 2, 1) / z).astype(np.float32),
        "offs": striped(idx),
    }


def reference(qT, cT, doT, rw, qm, dom, offs):
    idx = unstriped(offs)
    pick = lambda x: x[:, idx].reshape(x.shape[0], B, N).transpose(1, 0, 2)
    cq = mxq(pick(f64(cT)), 1, "e4m3")
    a = mxq(f64(qT), 1, "e4m3").transpose(0, 2, 1) @ cq
    p = np.square(np.maximum(a, 0.0))
    dp = mxq(f64(doT), 1, "e5m2").transpose(0, 2, 1) @ cq
    ds = f64(rw) * dp * 2.0 * np.maximum(a, 0.0)
    dk = mxq(f64(qm), 1, "e4m3").transpose(0, 2, 1) @ mxq(ds, 1, "e5m2")
    dv = mxq(f64(dom), 1, "e5m2").transpose(0, 2, 1) @ mxq(f64(rw) * p, 1, "e4m3")
    gc = np.zeros((D, T))
    gc[:, idx] = (dk + dv).transpose(1, 0, 2).reshape(D, B * N)
    return gc

@@ -1,0 +1,265 @@
+from contextlib import ExitStack
+
+import concourse.mybir as mybir
+
+B, N, T, D, R = 2, 512, 2048, 512, 512
+FLOPS = 4 * 2 * B * N * D * R
+
+F32 = mybir.dt.float32
+BF16 = mybir.dt.bfloat16
+U32 = mybir.dt.uint32
+U16 = mybir.dt.uint16
+U8 = mybir.dt.uint8
+E4M3 = mybir.dt.float8_e4m3fn_x4
+E5M2 = mybir.dt.float8_e5m2_x4
+COPY = mybir.ActivationFunctionType.Copy
+MULT = mybir.AluOpType.mult
+ADD = mybir.AluOpType.add
+MAX = mybir.AluOpType.max
+
+P = 128
+PACK = 4
+LIST_COLS = N // 16
+
+
+def tile_attend_gat_c_kernel(tc, qT, cT, doT, rw, qm, dom, offs, out):
+    nc = tc.nc
+
+    def cast(engine, dst, src):
+        if engine == "v":
+            nc.vector.tensor_copy(out=dst, in_=src)
+        elif engine == "s":
+            nc.scalar.activation(out=dst, in_=src, func=COPY)
+        else:
+            nc.gpsimd.tensor_scalar(out=dst, in0=src, scalar1=1.0, scalar2=0.0, op0=MULT, op1=ADD)
+
+    with ExitStack() as ctx:
+        keep = ctx.enter_context(tc.tile_pool(name="keep", bufs=1))
+        raw = ctx.enter_context(tc.tile_pool(name="raw", bufs=8))
+        stage = ctx.enter_context(tc.tile_pool(name="stage", bufs=4))
+        res = ctx.enter_context(tc.tile_pool(name="res", bufs=8))
+        psum = ctx.enter_context(tc.psum_pool(name="psum", bufs=4))
+
+        def mx_tiles(name):
+            codes = keep.tile([P, 512], U32, name=name + "_codes", align_bytes=64)
+            scales = keep.tile([P, 512], U8, name=name + "_scales", align_bytes=64)
+            return codes, scales
+
+        def quantize(operand, fmt, src, c0, c1):
+            codes, scales = operand
+            nc.vector.quantize_mx(out=codes[:, c0:c1].bitcast(fmt), scales=scales[:, c0:c1],
+                                  in_=src[:, PACK * c0:PACK * c1])
+
+        def load_rows(src):
+            t = raw.tile([P, PACK, 512], F32, name="rows", tag="raw")
+            nc.sync.dma_start(out=t[:], in_=src.rearrange("(p j) w -> p j w", j=PACK))
+            return t
+
+        gate = keep.tile([P, B, PACK], F32, name="gate")
+        nc.sync.dma_start(out=gate[:], in_=rw.rearrange("b (p j) o -> p b (j o)", j=PACK))
+        c_rows = cT.rearrange("(p j) t -> p j t", j=PACK)
+        H = T // 2
+        c_raw = {}
+        offsets = keep.tile([P, B * LIST_COLS], U16, name="offsets")
+        for u in range(2):
+            for h in range(2):
+                t = raw.tile([P, 2, H], F32, name="c_raw", tag="raw")
+                nc.sync.dma_start(out=t[:], in_=c_rows[:, 2 * u:2 * u + 2, h * H:(h + 1) * H])
+                c_raw[u, h] = t
+                if (u, h) == (0, 0):
+                    nc.sync.dma_start(offsets[:], offs)
+        rows = {}
+        for name, src in (("q", qT), ("do", doT), ("qm", qm), ("dom", dom)):
+            rows[name, 0] = load_rows(src[0])
+
+        gate2 = keep.tile([P, B, PACK], F32, name="gate2")
+        nc.scalar.activation(out=gate2[:], in_=gate[:], func=COPY, scale=2.0)
+
+        windows = [keep.tile([P, T], F32, name="window%d" % j) for j in range(4)]
+        for j, w in enumerate(windows):
+            (nc.vector if j < 2 else nc.gpsimd).memset(w[:], 0.0)
+
+        pool = [keep.tile([P, 2 * T], BF16, name="pool%d" % u) for u in range(2)]
+
+        def cast_pool(engine, u, h, c0, c1):
+            dst = pool[u][:, 2 * (h * H + c0):2 * (h * H + c1)].rearrange("p (c i e) -> p c e i", i=4, e=2)
+            src = c_raw[u, h][:, :, c0:c1].rearrange("p e (c i) -> p c e i", i=4)
+            cast(engine, dst, src)
+
+        picked = [keep.tile([P, PACK * N], BF16, name="picked%d" % b, align_bytes=64) for b in range(B)]
+
+        def gather(b, u):
+            nc.vector.tensor_copy(
+                out=picked[b][:].bitcast(U32)[:, u:2 * N:2],
+                in_=pool[u][:].bitcast(U32).indirect(offsets[:, b * LIST_COLS:(b + 1) * LIST_COLS]))
+
+        def cast_turned(engine, dst, src, m0, m1):
+            cast(engine,
+                 dst[:].rearrange("p (t m j) -> p m t j", t=PACK, j=PACK)[:, m0:m1],
+                 src[:].rearrange("p j (m t) -> p m t j", t=PACK)[:, m0:m1])
+
+        def cast_plain(engine, dst, src, c0, c1):
+            cast(engine,
+                 dst[:, PACK * c0:PACK * c1].rearrange("p (c i j) -> p c j i", i=4, j=PACK),
+                 src[:, :, c0:c1].rearrange("p j (c i) -> p c j i", i=4))
+
+        def staged():
+            return stage.tile([P, PACK * 512], BF16, name="staged", align_bytes=64)
+
+        cast_pool("s", 0, 0, 0, H)
+        cast_pool("s", 0, 1, 0, H)
+        gather(0, 0)
+        gather(1, 0)
+        cast_pool("s", 1, 0, 0, H)
+        cast_pool("v", 1, 1, 0, 640)
+        cast_pool("s", 1, 1, 640, H)
+        for name, src in (("q", qT), ("do", doT), ("qm", qm), ("dom", dom)):
+            rows[name, 1] = load_rows(src[1])
+
+        c_mx = [mx_tiles("c%d" % b) for b in range(B)]
+        gather(0, 1)
+        quantize(c_mx[0], E4M3, picked[0], 0, 512)
+
+        def turned_operand(name, b, fmt, shares):
+            mx = mx_tiles("%s%d" % (name, b))
+            g = staged()
+            for engine, m0, m1 in shares:
+                cast_turned(engine, g, rows[name, b], m0, m1)
+            quantize(mx, fmt, g, 0, 512)
+            return mx
+
+        def scores(b, q_mx):
+            banks = []
+            for c in range(4):
+                bank = psum.tile([P, PACK, P], F32, name="a", tag="a")
+                for t in range(PACK):
+                    nc.tensor.matmul_mx(
+                        out=bank[:, t, :],
+                        lhsT=q_mx[0][:, t * P:(t + 1) * P].bitcast(E4M3), lhsT_scale=q_mx[1][:, t * P:(t + 1) * P],
+                        rhs=c_mx[b][0][:, c * P:(c + 1) * P].bitcast(E4M3), rhs_scale=c_mx[b][1][:, c * P:(c + 1) * P],
+                        start=True, stop=True)
+                banks.append(bank)
+            return banks
+
+        def dscores(b, do_mx):
+            banks = []
+            for t in range(PACK):
+                bank = psum.tile([P, N], F32, name="dp", tag="wide")
+                nc.tensor.matmul_mx(
+                    out=bank[:],
+                    lhsT=do_mx[0][:, t * P:(t + 1) * P].bitcast(E5M2), lhsT_scale=do_mx[1][:, t * P:(t + 1) * P],
+                    rhs=c_mx[b][0][:].bitcast(E4M3), rhs_scale=c_mx[b][1][:],
+                    start=True, stop=True)
+                banks.append(bank)
+            return banks
+
+        ga = keep.tile([P, PACK, N], F32, name="ga")
+        gdp = keep.tile([P, PACK, N], F32, name="gdp")
+        pw = keep.tile([P, PACK * N], BF16, name="pw", align_bytes=64)
+        ds = keep.tile([P, PACK * N], BF16, name="ds", align_bytes=64)
+
+        def gated_a(b, a_banks, c):
+            for t in range(PACK):
+                nc.scalar.activation(out=ga[:, t, c * P:(c + 1) * P], in_=a_banks[c][:, t, :], func=COPY,
+                                     scale=gate[:, b, t:t + 1])
+
+        def gated_dp(b, dp_banks, t, engine):
+            if engine == "s":
+                nc.scalar.activation(out=gdp[:, t, :], in_=dp_banks[t][:], func=COPY, scale=gate2[:, b, t:t + 1])
+            else:
+                nc.vector.tensor_scalar(out=gdp[:, t, :], in0=dp_banks[t][:], scalar1=gate2[:, b, t:t + 1],
+                                        scalar2=None, op0=MULT)
+
+        def relu_times(dst, a_banks, other, c):
+            nc.vector.scalar_tensor_tensor(
+                out=dst[:, PACK * c * P:PACK * (c + 1) * P].rearrange("p (n t) -> p n t", t=PACK),
+                in0=a_banks[c][:].rearrange("p t n -> p n t"), scalar=0.0,
+                in1=other[:, :, c * P:(c + 1) * P].rearrange("p t n -> p n t"),
+                op0=MAX, op1=MULT)
+
+        def plain_operand(name, b, fmt, shares):
+            mx = mx_tiles("%s%d" % (name, b))
+            g = staged()
+            steps = []
+            for pieces, c0, c1 in shares:
+                steps.append((g, mx, fmt, rows[name, b], pieces, c0, c1))
+            return mx, steps
+
+        def run_step(step):
+            g, mx, fmt, src, pieces, c0, c1 = step
+            for engine, e0, e1 in pieces:
+                cast_plain(engine, g, src, e0, e1)
+            quantize(mx, fmt, g, c0, c1)
+
+        def gradient(b, j, qm_mx, ds_mx, dom_mx, pw_mx):
+            cols = slice(j * P, (j + 1) * P)
+            bank = psum.tile([P, N], F32, name="grad", tag="wide")
+            nc.tensor.matmul_mx(out=bank[:], lhsT=dom_mx[0][:, cols].bitcast(E5M2), lhsT_scale=dom_mx[1][:, cols],
+                                rhs=pw_mx[0][:].bitcast(E4M3), rhs_scale=pw_mx[1][:], start=True, stop=False)
+            nc.tensor.matmul_mx(out=bank[:], lhsT=qm_mx[0][:, cols].bitcast(E4M3), lhsT_scale=qm_mx[1][:, cols],
+                                rhs=ds_mx[0][:].bitcast(E5M2), rhs_scale=ds_mx[1][:], start=False, stop=True)
+            g = res.tile([P, N], F32, name="result")
+            nc.scalar.activation(out=g[:], in_=bank[:], func=COPY)
+            return g
+
+        def scatter(b, j, g):
+            nc.vector.tensor_copy(out=windows[j][:].indirect(offsets[:, b * LIST_COLS:(b + 1) * LIST_COLS]), in_=g[:])
+
+        EARLY = [([("g", 0, 128)], 0, 128), ([("g", 128, 256)], 128, 256), ([("g", 256, 384), ("g", 384, 512)], 256, 512)]
+        q_mx = turned_operand("q", 0, E4M3, [("s", 0, 128)])
+        a_banks = scores(0, q_mx)
+        do_mx = turned_operand("do", 0, E5M2, [("s", 0, 64), ("v", 64, 128)])
+        dp_banks = dscores(0, do_mx)
+        pw_mx, ds_mx = mx_tiles("pw0"), mx_tiles("ds0")
+        for c in range(4):
+            gated_a(0, a_banks, c)
+            relu_times(pw, a_banks, ga, c)
+        for t in range(PACK):
+            gated_dp(0, dp_banks, t, "vsvs"[t])
+        quantize(pw_mx, E4M3, pw, 0, 512)
+        qm_mx, qm_steps = plain_operand("qm", 0, E4M3, EARLY)
+        dom_mx, dom_steps = plain_operand("dom", 0, E5M2, EARLY)
+        for c in range(4):
+            relu_times(ds, a_banks, gdp, c)
+        run_step(qm_steps[0])
+        run_step(dom_steps[0])
+        quantize(ds_mx, E5M2, ds, 0, 512)
+        grads = {}
+        grads[0, 0] = gradient(0, 0, qm_mx, ds_mx, dom_mx, pw_mx)
+        run_step(qm_steps[1])
+        run_step(dom_steps[1])
+        grads[0, 1] = gradient(0, 1, qm_mx, ds_mx, dom_mx, pw_mx)
+        gather(1, 1)
+        quantize(c_mx[1], E4M3, picked[1], 0, 512)
+        run_step(qm_steps[2])
+        run_step(dom_steps[2])
+        grads[0, 2] = gradient(0, 2, qm_mx, ds_mx, dom_mx, pw_mx)
+        grads[0, 3] = gradient(0, 3, qm_mx, ds_mx, dom_mx, pw_mx)
+
+        q_mx = turned_operand("q", 1, E4M3, [("s", 0, 128)])
+        do_mx = turned_operand("do", 1, E5M2, [("s", 0, 128)])
+        a_banks = scores(1, q_mx)
+        dp_banks = dscores(1, do_mx)
+        pw_mx, ds_mx = mx_tiles("pw1"), mx_tiles("ds1")
+        for t in range(PACK):
+            gated_dp(1, dp_banks, t, "s")
+        for c in range(4):
+            relu_times(ds, a_banks, gdp, c)
+        for c in range(4):
+            gated_a(1, a_banks, c)
+            relu_times(pw, a_banks, ga, c)
+        quantize(ds_mx, E5M2, ds, 0, 512)
+        quarters = [("g", 128 * k, 128 * (k + 1)) for k in range(4)]
+        qm_mx, qm_steps = plain_operand("qm", 1, E4M3, [(quarters, 0, 512)])
+        dom_mx, dom_steps = plain_operand("dom", 1, E5M2, [(quarters, 0, 512)])
+        run_step(qm_steps[0])
+        quantize(pw_mx, E4M3, pw, 0, 512)
+        run_step(dom_steps[0])
+        for j in range(4):
+            grads[1, j] = gradient(1, j, qm_mx, ds_mx, dom_mx, pw_mx)
+
+        for j in range(4):
+            scatter(0, j, grads[0, j])
+        for j in range(4):
+            scatter(1, j, grads[1, j])
+            nc.sync.dma_start(out=out[j * P:(j + 1) * P, :], in_=windows[j][:])

@@ -20,6 +20,14 @@ MAX = mybir.AluOpType.max
 P = 128
 PACK = 4
 LIST_COLS = N // 16
+LATE = False
+C01 = "v"
+C11 = 640
+DO0B = "v"
+Y0 = "vsvs"
+DP_BANK = [[0, 1, 2, 3], [0, 3, 1, 2]]
+GRAD_BANK = [["w0", "w1", "w2", "a1"], ["w0", "w1", "w2", "w3"]]
+TAG = {"r_q1": "r_c00", "r_do1": "r_c01", "r_qm1": "r_c10", "r_dom1": "r_c11", "s_pair2": "gdp0", "s_qm1": "gdp0", "s_pair0": "ga0", "s_do1": "gdp0", "res10": "r_c10", "s_pair3": "r_c01", "pw0": "s_q0", "s_dom1": "ga1", "s_q1": "r_do0", "res13": "r_c11", "res02": "res00"}
 
 
 def tile_attend_gat_c_kernel(tc, qT, cT, doT, rw, qm, dom, offs, out):
@@ -35,10 +43,11 @@ def tile_attend_gat_c_kernel(tc, qT, cT, doT, rw, qm, dom, offs, out):
 
     with ExitStack() as ctx:
         keep = ctx.enter_context(tc.tile_pool(name="keep", bufs=1))
-        raw = ctx.enter_context(tc.tile_pool(name="raw", bufs=8))
-        stage = ctx.enter_context(tc.tile_pool(name="stage", bufs=4))
-        res = ctx.enter_context(tc.tile_pool(name="res", bufs=8))
-        psum = ctx.enter_context(tc.psum_pool(name="psum", bufs=4))
+        work = ctx.enter_context(tc.tile_pool(name="work", bufs=1))
+        psum = ctx.enter_context(tc.psum_pool(name="psum", bufs=1))
+
+        def work_tile(name, shape, dtype):
+            return work.tile(shape, dtype, name=name, tag=TAG.get(name, name), align_bytes=64)
 
         def mx_tiles(name):
             codes = keep.tile([P, 512], U32, name=name + "_codes", align_bytes=64)
@@ -47,12 +56,14 @@ def tile_attend_gat_c_kernel(tc, qT, cT, doT, rw, qm, dom, offs, out):
 
         def quantize(operand, fmt, src, c0, c1):
             codes, scales = operand
-            nc.vector.quantize_mx(out=codes[:, c0:c1].bitcast(fmt), scales=scales[:, c0:c1],
-                                  in_=src[:, PACK * c0:PACK * c1])
+            nc.vector.quantize_mx(out=codes[:, c0:c1].bitcast(fmt), scales=scales[:, c0:c1], in_=src)
 
-        def load_rows(src):
-            t = raw.tile([P, PACK, 512], F32, name="rows", tag="raw")
-            nc.sync.dma_start(out=t[:], in_=src.rearrange("(p j) w -> p j w", j=PACK))
+        def load_rows(name, src, pieces=1):
+            t = work_tile(name, [P, PACK, 512], F32)
+            view = src.rearrange("(p j) w -> p j w", j=PACK)
+            w = 512 // pieces
+            for k in range(pieces):
+                nc.sync.dma_start(out=t[:, :, k * w:(k + 1) * w], in_=view[:, :, k * w:(k + 1) * w])
             return t
 
         gate = keep.tile([P, B, PACK], F32, name="gate")
@@ -63,14 +74,14 @@ def tile_attend_gat_c_kernel(tc, qT, cT, doT, rw, qm, dom, offs, out):
         offsets = keep.tile([P, B * LIST_COLS], U16, name="offsets")
         for u in range(2):
             for h in range(2):
-                t = raw.tile([P, 2, H], F32, name="c_raw", tag="raw")
+                t = work_tile("r_c%d%d" % (u, h), [P, 2, H], F32)
                 nc.sync.dma_start(out=t[:], in_=c_rows[:, 2 * u:2 * u + 2, h * H:(h + 1) * H])
                 c_raw[u, h] = t
                 if (u, h) == (0, 0):
                     nc.sync.dma_start(offsets[:], offs)
         rows = {}
         for name, src in (("q", qT), ("do", doT), ("qm", qm), ("dom", dom)):
-            rows[name, 0] = load_rows(src[0])
+            rows[name, 0] = load_rows("r_%s0" % name, src[0], 2 if name in ("q", "do") else 1)
 
         gate2 = keep.tile([P, B, PACK], F32, name="gate2")
         nc.scalar.activation(out=gate2[:], in_=gate[:], func=COPY, scale=2.0)
@@ -86,84 +97,85 @@ def tile_attend_gat_c_kernel(tc, qT, cT, doT, rw, qm, dom, offs, out):
             src = c_raw[u, h][:, :, c0:c1].rearrange("p e (c i) -> p c e i", i=4)
             cast(engine, dst, src)
 
-        picked = [keep.tile([P, PACK * N], BF16, name="picked%d" % b, align_bytes=64) for b in range(B)]
-
-        def gather(b, u):
+        def gather(b, u, dst):
             nc.vector.tensor_copy(
-                out=picked[b][:].bitcast(U32)[:, u:2 * N:2],
-                in_=pool[u][:].bitcast(U32).indirect(offsets[:, b * LIST_COLS:(b + 1) * LIST_COLS]))
+                out=dst, in_=pool[u][:].bitcast(U32).indirect(offsets[:, b * LIST_COLS:(b + 1) * LIST_COLS]))
 
         def cast_turned(engine, dst, src, m0, m1):
             cast(engine,
-                 dst[:].rearrange("p (t m j) -> p m t j", t=PACK, j=PACK)[:, m0:m1],
-                 src[:].rearrange("p j (m t) -> p m t j", t=PACK)[:, m0:m1])
+                 dst[:].rearrange("p (t m j) -> p m j t", t=PACK, j=PACK)[:, m0:m1],
+                 src[:].rearrange("p j (m t) -> p m j t", t=PACK)[:, m0:m1])
 
         def cast_plain(engine, dst, src, c0, c1):
             cast(engine,
-                 dst[:, PACK * c0:PACK * c1].rearrange("p (c i j) -> p c j i", i=4, j=PACK),
+                 dst.rearrange("p (c i j) -> p c j i", i=4, j=PACK),
                  src[:, :, c0:c1].rearrange("p j (c i) -> p c j i", i=4))
 
-        def staged():
-            return stage.tile([P, PACK * 512], BF16, name="staged", align_bytes=64)
+        mx = {}
+        FMT = {"c": E4M3, "q": E4M3, "do": E5M2, "qm": E4M3, "dom": E5M2, "pw": E4M3, "ds": E5M2}
 
-        cast_pool("s", 0, 0, 0, H)
-        cast_pool("s", 0, 1, 0, H)
-        gather(0, 0)
-        gather(1, 0)
-        cast_pool("s", 1, 0, 0, H)
-        cast_pool("v", 1, 1, 0, 640)
-        cast_pool("s", 1, 1, 640, H)
-        for name, src in (("q", qT), ("do", doT), ("qm", qm), ("dom", dom)):
-            rows[name, 1] = load_rows(src[1])
+        def quant(name, b, src, c0=0, c1=512):
+            if (name, b) not in mx:
+                mx[name, b] = mx_tiles("%s%d" % (name, b))
+            quantize(mx[name, b], FMT[name], src, c0, c1)
 
-        c_mx = [mx_tiles("c%d" % b) for b in range(B)]
-        gather(0, 1)
-        quantize(c_mx[0], E4M3, picked[0], 0, 512)
+        def matmul(dst, left, lcols, right, rcols, start, stop):
+            nc.tensor.matmul_mx(
+                out=dst,
+                lhsT=mx[left][0][:, lcols].bitcast(FMT[left[0]]), lhsT_scale=mx[left][1][:, lcols],
+                rhs=mx[right][0][:, rcols].bitcast(FMT[right[0]]), rhs_scale=mx[right][1][:, rcols],
+                start=start, stop=stop)
 
-        def turned_operand(name, b, fmt, shares):
-            mx = mx_tiles("%s%d" % (name, b))
-            g = staged()
+        def block(k):
+            return slice(k * P, (k + 1) * P)
+
+        def turned(name, b, shares):
+            g = work_tile("s_%s%d" % (name, b), [P, PACK * 512], BF16)
             for engine, m0, m1 in shares:
                 cast_turned(engine, g, rows[name, b], m0, m1)
-            quantize(mx, fmt, g, 0, 512)
-            return mx
+            return g
 
-        def scores(b, q_mx):
+        def plain(name, b, engine, step=128):
+            g = work_tile("s_%s%d" % (name, b), [P, PACK * 512], BF16)
+            for c0 in range(0, 512, step):
+                cast_plain(engine, g[:, PACK * c0:PACK * (c0 + step)], rows[name, b], c0, c0 + step)
+            return g
+
+        def pair_cast(j0, j1, engine):
+            w = (j1 - j0) * P
+            g = work_tile("s_pair%d" % j0, [P, 2, PACK * w], BF16)
+            for k, name in enumerate(("dom", "qm")):
+                for j in range(j0, j1):
+                    cast_plain(engine, g[:, k, PACK * P * (j - j0):PACK * P * (j + 1 - j0)], rows[name, 0], j * P, (j + 1) * P)
+            return g
+
+        def pair_quant(j0, j1, g):
+            for k, name in enumerate(("dom", "qm")):
+                quant(name, 0, g[:, k, :], j0 * P, j1 * P)
+
+        def scores(b):
             banks = []
             for c in range(4):
-                bank = psum.tile([P, PACK, P], F32, name="a", tag="a")
+                bank = psum.tile([P, PACK, P], F32, name="a%d" % c, tag="a%d" % c)
                 for t in range(PACK):
-                    nc.tensor.matmul_mx(
-                        out=bank[:, t, :],
-                        lhsT=q_mx[0][:, t * P:(t + 1) * P].bitcast(E4M3), lhsT_scale=q_mx[1][:, t * P:(t + 1) * P],
-                        rhs=c_mx[b][0][:, c * P:(c + 1) * P].bitcast(E4M3), rhs_scale=c_mx[b][1][:, c * P:(c + 1) * P],
-                        start=True, stop=True)
+                    matmul(bank[:, t, :], ("q", b), block(t), ("c", b), block(c), True, True)
                 banks.append(bank)
             return banks
 
-        def dscores(b, do_mx):
+        def dscores(b):
             banks = []
             for t in range(PACK):
-                bank = psum.tile([P, N], F32, name="dp", tag="wide")
-                nc.tensor.matmul_mx(
-                    out=bank[:],
-                    lhsT=do_mx[0][:, t * P:(t + 1) * P].bitcast(E5M2), lhsT_scale=do_mx[1][:, t * P:(t + 1) * P],
-                    rhs=c_mx[b][0][:].bitcast(E4M3), rhs_scale=c_mx[b][1][:],
-                    start=True, stop=True)
+                bank = psum.tile([P, N], F32, name="dp%d" % t, tag="w%d" % DP_BANK[b][t])
+                matmul(bank[:], ("do", b), block(t), ("c", b), slice(0, N), True, True)
                 banks.append(bank)
             return banks
 
-        ga = keep.tile([P, PACK, N], F32, name="ga")
-        gdp = keep.tile([P, PACK, N], F32, name="gdp")
-        pw = keep.tile([P, PACK * N], BF16, name="pw", align_bytes=64)
-        ds = keep.tile([P, PACK * N], BF16, name="ds", align_bytes=64)
-
-        def gated_a(b, a_banks, c):
+        def gated_a(b, ga, a_banks, c):
             for t in range(PACK):
-                nc.scalar.activation(out=ga[:, t, c * P:(c + 1) * P], in_=a_banks[c][:, t, :], func=COPY,
+                nc.scalar.activation(out=ga[:, t, block(c)], in_=a_banks[c][:, t, :], func=COPY,
                                      scale=gate[:, b, t:t + 1])
 
-        def gated_dp(b, dp_banks, t, engine):
+        def gated_dp(b, gdp, dp_banks, t, engine):
             if engine == "s":
                 nc.scalar.activation(out=gdp[:, t, :], in_=dp_banks[t][:], func=COPY, scale=gate2[:, b, t:t + 1])
             else:
@@ -174,92 +186,107 @@ def tile_attend_gat_c_kernel(tc, qT, cT, doT, rw, qm, dom, offs, out):
             nc.vector.scalar_tensor_tensor(
                 out=dst[:, PACK * c * P:PACK * (c + 1) * P].rearrange("p (n t) -> p n t", t=PACK),
                 in0=a_banks[c][:].rearrange("p t n -> p n t"), scalar=0.0,
-                in1=other[:, :, c * P:(c + 1) * P].rearrange("p t n -> p n t"),
+                in1=other[:, :, block(c)].rearrange("p t n -> p n t"),
                 op0=MAX, op1=MULT)
 
-        def plain_operand(name, b, fmt, shares):
-            mx = mx_tiles("%s%d" % (name, b))
-            g = staged()
-            steps = []
-            for pieces, c0, c1 in shares:
-                steps.append((g, mx, fmt, rows[name, b], pieces, c0, c1))
-            return mx, steps
+        def gradients(b, js):
+            banks = {}
+            for j in js:
+                banks[j] = psum.tile([P, N], F32, name="grad%d%d" % (b, j), tag=GRAD_BANK[b][j])
+                matmul(banks[j][:], ("dom", b), block(j), ("pw", b), slice(0, N), True, False)
+            for j in js:
+                matmul(banks[j][:], ("qm", b), block(j), ("ds", b), slice(0, N), False, True)
+                grads[b, j] = work_tile("res%d%d" % (b, j), [P, N], F32)
+                nc.scalar.activation(out=grads[b, j][:], in_=banks[j][:], func=COPY)
 
-        def run_step(step):
-            g, mx, fmt, src, pieces, c0, c1 = step
-            for engine, e0, e1 in pieces:
-                cast_plain(engine, g, src, e0, e1)
-            quantize(mx, fmt, g, c0, c1)
+        def scatter(b, j):
+            nc.vector.tensor_copy(out=windows[j][:].indirect(offsets[:, b * LIST_COLS:(b + 1) * LIST_COLS]),
+                                  in_=grads[b, j][:])
 
-        def gradient(b, j, qm_mx, ds_mx, dom_mx, pw_mx):
-            cols = slice(j * P, (j + 1) * P)
-            bank = psum.tile([P, N], F32, name="grad", tag="wide")
-            nc.tensor.matmul_mx(out=bank[:], lhsT=dom_mx[0][:, cols].bitcast(E5M2), lhsT_scale=dom_mx[1][:, cols],
-                                rhs=pw_mx[0][:].bitcast(E4M3), rhs_scale=pw_mx[1][:], start=True, stop=False)
-            nc.tensor.matmul_mx(out=bank[:], lhsT=qm_mx[0][:, cols].bitcast(E4M3), lhsT_scale=qm_mx[1][:, cols],
-                                rhs=ds_mx[0][:].bitcast(E5M2), rhs_scale=ds_mx[1][:], start=False, stop=True)
-            g = res.tile([P, N], F32, name="result")
-            nc.scalar.activation(out=g[:], in_=bank[:], func=COPY)
-            return g
-
-        def scatter(b, j, g):
-            nc.vector.tensor_copy(out=windows[j][:].indirect(offsets[:, b * LIST_COLS:(b + 1) * LIST_COLS]), in_=g[:])
-
-        EARLY = [([("g", 0, 128)], 0, 128), ([("g", 128, 256)], 128, 256), ([("g", 256, 384), ("g", 384, 512)], 256, 512)]
-        q_mx = turned_operand("q", 0, E4M3, [("s", 0, 128)])
-        a_banks = scores(0, q_mx)
-        do_mx = turned_operand("do", 0, E5M2, [("s", 0, 64), ("v", 64, 128)])
-        dp_banks = dscores(0, do_mx)
-        pw_mx, ds_mx = mx_tiles("pw0"), mx_tiles("ds0")
-        for c in range(4):
-            gated_a(0, a_banks, c)
-            relu_times(pw, a_banks, ga, c)
-        for t in range(PACK):
-            gated_dp(0, dp_banks, t, "vsvs"[t])
-        quantize(pw_mx, E4M3, pw, 0, 512)
-        qm_mx, qm_steps = plain_operand("qm", 0, E4M3, EARLY)
-        dom_mx, dom_steps = plain_operand("dom", 0, E5M2, EARLY)
-        for c in range(4):
-            relu_times(ds, a_banks, gdp, c)
-        run_step(qm_steps[0])
-        run_step(dom_steps[0])
-        quantize(ds_mx, E5M2, ds, 0, 512)
         grads = {}
-        grads[0, 0] = gradient(0, 0, qm_mx, ds_mx, dom_mx, pw_mx)
-        run_step(qm_steps[1])
-        run_step(dom_steps[1])
-        grads[0, 1] = gradient(0, 1, qm_mx, ds_mx, dom_mx, pw_mx)
-        gather(1, 1)
-        quantize(c_mx[1], E4M3, picked[1], 0, 512)
-        run_step(qm_steps[2])
-        run_step(dom_steps[2])
-        grads[0, 2] = gradient(0, 2, qm_mx, ds_mx, dom_mx, pw_mx)
-        grads[0, 3] = gradient(0, 3, qm_mx, ds_mx, dom_mx, pw_mx)
+        quarters = [("s", 32 * k, 32 * (k + 1)) for k in range(4)]
+        picked0 = work_tile("picked0", [P, PACK * N], BF16)
+        cast_pool("s", 0, 0, 0, H)
+        cast_pool(C01, 0, 1, 0, H)
+        gather(0, 0, picked0[:].bitcast(U32)[:, 0:2 * N:2])
+        if LATE:
+            half0 = work_tile("half0", [P, 2 * N], BF16)
+            gather(1, 0, half0[:].bitcast(U32))
+        else:
+            picked1 = work_tile("picked1", [P, PACK * N], BF16)
+            gather(1, 0, picked1[:].bitcast(U32)[:, 0:2 * N:2])
+        cast_pool("s", 1, 0, 0, H)
+        if C11:
+            cast_pool("v", 1, 1, 0, C11)
+        cast_pool("s", 1, 1, C11, H)
+        for name, src in (("q", qT), ("do", doT), ("qm", qm), ("dom", dom)):
+            rows[name, 1] = load_rows("r_%s1" % name, src[1])
+        gather(0, 1, picked0[:].bitcast(U32)[:, 1:2 * N:2])
+        quant("c", 0, picked0[:])
+        if not LATE:
+            gather(1, 1, picked1[:].bitcast(U32)[:, 1:2 * N:2])
+            quant("c", 1, picked1[:])
 
-        q_mx = turned_operand("q", 1, E4M3, [("s", 0, 128)])
-        do_mx = turned_operand("do", 1, E5M2, [("s", 0, 128)])
-        a_banks = scores(1, q_mx)
-        dp_banks = dscores(1, do_mx)
-        pw_mx, ds_mx = mx_tiles("pw1"), mx_tiles("ds1")
+        quant("q", 0, turned("q", 0, [("s", 0, 64), ("s", 64, 128)])[:])
+        a_banks = scores(0)
+        quant("do", 0, turned("do", 0, [("s", 0, 64), (DO0B, 64, 128)])[:])
+        dp_banks = dscores(0)
+        ga = work_tile("ga0", [P, PACK, N], F32)
+        gdp = work_tile("gdp0", [P, PACK, N], F32)
+        pw = work_tile("pw0", [P, PACK * N], BF16)
+        ds = work_tile("ds0", [P, PACK * N], BF16)
+        for c in range(4):
+            gated_a(0, ga, a_banks, c)
+            relu_times(pw, a_banks, ga, c)
         for t in range(PACK):
-            gated_dp(1, dp_banks, t, "s")
+            gated_dp(0, gdp, dp_banks, t, Y0[t])
+        quant("pw", 0, pw[:])
+        first = pair_cast(0, 2, "s")
         for c in range(4):
             relu_times(ds, a_banks, gdp, c)
+        pair_quant(0, 2, first)
+        quant("ds", 0, ds[:])
+        s_q1 = turned("q", 1, quarters)
+        if LATE:
+            half1 = work_tile("half1", [P, 2 * N], BF16)
+            gather(1, 1, half1[:].bitcast(U32))
+        gradients(0, [0, 1])
+        quant("q", 1, s_q1[:])
+        if LATE:
+            picked1 = work_tile("picked1", [P, PACK * N], BF16)
+            for u, half in enumerate((half0, half1)):
+                nc.scalar.copy(out=picked1[:].rearrange("p (n u e) -> p n u e", u=2, e=2)[:, :, u, :],
+                               in_=half[:].rearrange("p (n e) -> p n e", e=2))
+        scatter(0, 0)
+        if LATE:
+            quant("c", 1, picked1[:])
+        a_banks = scores(1)
+        pair_quant(2, 3, pair_cast(2, 3, "s"))
+        s_do1 = turned("do", 1, quarters)
+        scatter(0, 1)
+        gradients(0, [2])
+        quant("do", 1, s_do1[:])
+        dp_banks = dscores(1)
+        scatter(0, 2)
+        ga = work_tile("ga1", [P, PACK, N], F32)
+        gdp = work_tile("gdp1", [P, PACK, N], F32)
+        pw = work_tile("pw1", [P, PACK * N], BF16)
+        ds = work_tile("ds1", [P, PACK * N], BF16)
         for c in range(4):
-            gated_a(1, a_banks, c)
+            gated_a(1, ga, a_banks, c)
             relu_times(pw, a_banks, ga, c)
-        quantize(ds_mx, E5M2, ds, 0, 512)
-        quarters = [("g", 128 * k, 128 * (k + 1)) for k in range(4)]
-        qm_mx, qm_steps = plain_operand("qm", 1, E4M3, [(quarters, 0, 512)])
-        dom_mx, dom_steps = plain_operand("dom", 1, E5M2, [(quarters, 0, 512)])
-        run_step(qm_steps[0])
-        quantize(pw_mx, E4M3, pw, 0, 512)
-        run_step(dom_steps[0])
+        for t in range(PACK):
+            gated_dp(1, gdp, dp_banks, t, "s")
+        quant("pw", 1, pw[:])
+        for c in range(4):
+            relu_times(ds, a_banks, gdp, c)
+        pair_quant(3, 4, pair_cast(3, 4, "s"))
+        quant("qm", 1, plain("qm", 1, "s")[:])
+        quant("dom", 1, plain("dom", 1, "s")[:])
+        quant("ds", 1, ds[:])
+        gradients(0, [3])
+        gradients(1, [0, 1, 2, 3])
+        scatter(0, 3)
         for j in range(4):
-            grads[1, j] = gradient(1, j, qm_mx, ds_mx, dom_mx, pw_mx)
-
-        for j in range(4):
-            scatter(0, j, grads[0, j])
-        for j in range(4):
-            scatter(1, j, grads[1, j])
+            scatter(1, j)
             nc.sync.dma_start(out=out[j * P:(j + 1) * P, :], in_=windows[j][:])

@@ -12,6 +12,8 @@ U16 = mybir.dt.uint16
 U8 = mybir.dt.uint8
 E4M3 = mybir.dt.float8_e4m3fn_x4
 E5M2 = mybir.dt.float8_e5m2_x4
+RELU = mybir.ActivationFunctionType.Relu
+SQUARE = mybir.ActivationFunctionType.Square
 COPY = mybir.ActivationFunctionType.Copy
 MULT = mybir.AluOpType.mult
 ADD = mybir.AluOpType.add
@@ -20,273 +22,285 @@ MAX = mybir.AluOpType.max
 P = 128
 PACK = 4
 LIST_COLS = N // 16
-LATE = False
-C01 = "v"
-C11 = 640
-DO0B = "v"
-Y0 = "vsvs"
-DP_BANK = [[0, 1, 2, 3], [0, 3, 1, 2]]
-GRAD_BANK = [["w0", "w1", "w2", "a1"], ["w0", "w1", "w2", "w3"]]
-TAG = {"r_q1": "r_c00", "r_do1": "r_c01", "r_qm1": "r_c10", "r_dom1": "r_c11", "s_pair2": "gdp0", "s_qm1": "gdp0", "s_pair0": "ga0", "s_do1": "gdp0", "res10": "r_c10", "s_pair3": "r_c01", "pw0": "s_q0", "s_dom1": "ga1", "s_q1": "r_do0", "res13": "r_c11", "res02": "res00"}
+H = T // 2
+FMT = {"c": E4M3, "q": E4M3, "do": E5M2, "qm": E4M3, "dom": E5M2, "pw": E4M3, "ds": E5M2}
+GROUPS = [[(0, 2), (2, 3), (3, 4)], [(0, 4)]]
+HOST = "s_ds0"
+PLAIN = [False, True]
+SQ = [False, True]
+TAG = {"res03": "ga1", "s_qm1_0": "x_c1", "r_dom1": "e_q1", "grad11": "dp13", "gdp1": "x_do0", "a12": "dp02", "window1": "r_do0", "grad12": "a03", "s_pw0": "r_do0", "s_pw1": "x_do1", "a11": "a00", "grad10": "a03", "r_dom0": "r_c00", "gdp0": "r_q0", "s_do1": "x_q0", "ra1": "r_q0", "s_dom0_2": "r_do1", "s_dom1_0": "r_qm0", "res10": "x_qm1", "a13": "a03", "s_q1": "x_do0", "grad02": "a01", "grad03": "a00", "grad01": "a00", "dp11": "dp02", "grad13": "a01", "dp10": "dp00", "dp01": "dp02", "r_q1": "e_c0", "s_q0": "r_c01", "a10": "dp03", "res01": "r_c00", "dp12": "dp00", "grad00": "a01"}
+ENG = {"zero0": "v", "zero1": "g", "zero2": "g", "zero3": "g", "P000512": "v", "P005121024": "v", "P010512": "s", "P015121024": "v", "P100512": "s", "P105121024": "s", "P110256": "v", "P11256512": "v", "P11512768": "s", "P117681024": "v", "W1": "s", "Tq00": "v", "Tq01": "s", "Tq02": "s", "Tq03": "g", "Tdo00": "s", "Tdo01": "v", "Tdo02": "v", "Tdo03": "v", "Y00": "s", "Y01": "s", "Y02": "s", "Y03": "s", "Cdom0020": "s", "Cdom0021": "s", "Cqm0020": "g", "Cqm0021": "g", "O00": "v", "O01": "s", "Tq10": "s", "Tq11": "s", "Tq12": "s", "Tq13": "s", "Tdo10": "s", "Tdo11": "s", "Tdo12": "s", "Tdo13": "g", "Cdom0232": "s", "Cqm0232": "s", "Y10": "s", "Y11": "s", "Y12": "s", "Y13": "v", "O02": "s", "M10": "g", "M11": "g", "M12": "g", "M13": "g", "M14": "g", "M15": "g", "M16": "g", "M17": "g", "Cdom0343": "s", "Cqm0343": "s", "Cdom1040": "s", "Cdom1041": "s", "Cdom1042": "s", "Cdom1043": "s", "Cqm1040": "s", "Cqm1041": "s", "Cqm1042": "g", "Cqm1043": "s", "O03": "s", "O10": "s", "O11": "s", "O12": "s", "O13": "s"}
+ORDER = ["Lc00", "zero3", "Lc01", "list", "Lc10", "P100512", "Lc11", "gate", "P015121024", "P11256512", "P010512", "Lq0", "Tq01", "P000512", "P117681024", "Tq00", "Ldo0", "P105121024", "Tdo00", "P005121024", "Tq02", "P110256", "P11512768", "G01", "Tdo01", "Tq03", "Qq0", "G00", "Qc0", "A03", "Tdo02", "Tdo03", "X03", "Qdo0", "A01", "A00", "Ldo1", "Ldom0", "X01", "X00", "A02", "D02", "Cdom0021", "Epwga00", "Epwga03", "Y02", "Epwga01", "D01", "X02", "Y01", "D00", "Y00", "D03", "Epwga02", "Y03", "Lq1", "zero0", "Tdo11", "Edsgdp00", "Edsgdp01", "zero2", "Qpw0", "Tq13", "Tq11", "Tq10", "Edsgdp02", "Lqm0", "Cdom0020", "Cqm0021", "Tdo12", "Edsgdp03", "Tdo10", "Cqm0020", "Qds0", "Qqm002", "Tq12", "G10", "G11", "Tdo13", "Qdom002", "Qq1", "V00", "K00", "Cdom0232", "W1", "Qc1", "Qdo1", "V01", "K01", "D10", "D11", "Cdom0343", "Y10", "O01", "Y11", "A13", "A10", "Cqm0232", "A11", "D12", "R13", "D13", "R11", "O00", "Qdom023", "zero1", "Cqm0343", "R10", "Z01", "Y12", "S10", "V02", "Z00", "Y13", "A12", "Qqm023", "K02", "Ldom1", "Lqm1", "R12", "Cdom1043", "Cdom1041", "Edsgdp10", "Qdom034", "S12", "M14", "M11", "Edsgdp11", "Edsgdp12", "Edsgdp13", "S11", "V03", "S13", "Cdom1042", "M10", "M15", "O02", "M13", "Qqm034", "Qds1", "M17", "M12", "Cqm1042", "Z02", "M16", "K03", "Cqm1043", "Qpw1", "Cdom1040", "Cqm1041", "Qdom104", "V11", "Cqm1040", "V12", "Qqm104", "K12", "O03", "V13", "O12", "V10", "K11", "K10", "K13", "O11", "Z11", "St1", "Z03", "O10", "O13", "Z13", "Z12", "St3", "Z10", "St0", "St2"]
 
 
 def tile_attend_gat_c_kernel(tc, qT, cT, doT, rw, qm, dom, offs, out):
     nc = tc.nc
-
-    def cast(engine, dst, src):
-        if engine == "v":
-            nc.vector.tensor_copy(out=dst, in_=src)
-        elif engine == "s":
-            nc.scalar.activation(out=dst, in_=src, func=COPY)
-        else:
-            nc.gpsimd.tensor_scalar(out=dst, in0=src, scalar1=1.0, scalar2=0.0, op0=MULT, op1=ADD)
+    source = {"q": qT, "do": doT, "qm": qm, "dom": dom}
 
     with ExitStack() as ctx:
         keep = ctx.enter_context(tc.tile_pool(name="keep", bufs=1))
         work = ctx.enter_context(tc.tile_pool(name="work", bufs=1))
         psum = ctx.enter_context(tc.psum_pool(name="psum", bufs=1))
+        tiles = {}
+        steps = {}
 
-        def work_tile(name, shape, dtype):
-            return work.tile(shape, dtype, name=name, tag=TAG.get(name, name), align_bytes=64)
+        def tile(name, shape, dtype):
+            if name == HOST:
+                return tile("halves1", [P, 6 * N], BF16)[:, 2 * N:6 * N]
+            if name not in tiles:
+                tiles[name] = work.tile(shape, dtype, name=name, tag=TAG.get(name, name), align_bytes=64)
+            return tiles[name][:]
 
-        def mx_tiles(name):
-            codes = keep.tile([P, 512], U32, name=name + "_codes", align_bytes=64)
-            scales = keep.tile([P, 512], U8, name=name + "_scales", align_bytes=64)
-            return codes, scales
+        def bank(name, shape):
+            if name not in tiles:
+                tiles[name] = psum.tile(shape, F32, name=name, tag=TAG.get(name, name))
+            return tiles[name][:]
 
-        def quantize(operand, fmt, src, c0, c1):
-            codes, scales = operand
-            nc.vector.quantize_mx(out=codes[:, c0:c1].bitcast(fmt), scales=scales[:, c0:c1], in_=src)
+        def codes(name, b):
+            return tile("x_%s%d" % (name, b), [P, 512], U32)
 
-        def load_rows(name, src, pieces=1):
-            t = work_tile(name, [P, PACK, 512], F32)
-            view = src.rearrange("(p j) w -> p j w", j=PACK)
-            w = 512 // pieces
-            for k in range(pieces):
-                nc.sync.dma_start(out=t[:, :, k * w:(k + 1) * w], in_=view[:, :, k * w:(k + 1) * w])
-            return t
-
-        gate = keep.tile([P, B, PACK], F32, name="gate")
-        nc.sync.dma_start(out=gate[:], in_=rw.rearrange("b (p j) o -> p b (j o)", j=PACK))
-        c_rows = cT.rearrange("(p j) t -> p j t", j=PACK)
-        H = T // 2
-        c_raw = {}
-        offsets = keep.tile([P, B * LIST_COLS], U16, name="offsets")
-        for u in range(2):
-            for h in range(2):
-                t = work_tile("r_c%d%d" % (u, h), [P, 2, H], F32)
-                nc.sync.dma_start(out=t[:], in_=c_rows[:, 2 * u:2 * u + 2, h * H:(h + 1) * H])
-                c_raw[u, h] = t
-                if (u, h) == (0, 0):
-                    nc.sync.dma_start(offsets[:], offs)
-        rows = {}
-        for name, src in (("q", qT), ("do", doT), ("qm", qm), ("dom", dom)):
-            rows[name, 0] = load_rows("r_%s0" % name, src[0], 2 if name in ("q", "do") else 1)
-
-        gate2 = keep.tile([P, B, PACK], F32, name="gate2")
-        nc.scalar.activation(out=gate2[:], in_=gate[:], func=COPY, scale=2.0)
-
-        windows = [keep.tile([P, T], F32, name="window%d" % j) for j in range(4)]
-        for j, w in enumerate(windows):
-            (nc.vector if j < 2 else nc.gpsimd).memset(w[:], 0.0)
-
-        pool = [keep.tile([P, 2 * T], BF16, name="pool%d" % u) for u in range(2)]
-
-        def cast_pool(engine, u, h, c0, c1):
-            dst = pool[u][:, 2 * (h * H + c0):2 * (h * H + c1)].rearrange("p (c i e) -> p c e i", i=4, e=2)
-            src = c_raw[u, h][:, :, c0:c1].rearrange("p e (c i) -> p c e i", i=4)
-            cast(engine, dst, src)
-
-        def gather(b, u, dst):
-            nc.vector.tensor_copy(
-                out=dst, in_=pool[u][:].bitcast(U32).indirect(offsets[:, b * LIST_COLS:(b + 1) * LIST_COLS]))
-
-        def cast_turned(engine, dst, src, m0, m1):
-            cast(engine,
-                 dst[:].rearrange("p (t m j) -> p m j t", t=PACK, j=PACK)[:, m0:m1],
-                 src[:].rearrange("p j (m t) -> p m j t", t=PACK)[:, m0:m1])
-
-        def cast_plain(engine, dst, src, c0, c1):
-            cast(engine,
-                 dst.rearrange("p (c i j) -> p c j i", i=4, j=PACK),
-                 src[:, :, c0:c1].rearrange("p j (c i) -> p c j i", i=4))
-
-        mx = {}
-        FMT = {"c": E4M3, "q": E4M3, "do": E5M2, "qm": E4M3, "dom": E5M2, "pw": E4M3, "ds": E5M2}
-
-        def quant(name, b, src, c0=0, c1=512):
-            if (name, b) not in mx:
-                mx[name, b] = mx_tiles("%s%d" % (name, b))
-            quantize(mx[name, b], FMT[name], src, c0, c1)
-
-        def matmul(dst, left, lcols, right, rcols, start, stop):
-            nc.tensor.matmul_mx(
-                out=dst,
-                lhsT=mx[left][0][:, lcols].bitcast(FMT[left[0]]), lhsT_scale=mx[left][1][:, lcols],
-                rhs=mx[right][0][:, rcols].bitcast(FMT[right[0]]), rhs_scale=mx[right][1][:, rcols],
-                start=start, stop=stop)
+        def scales(name, b):
+            return tile("e_%s%d" % (name, b), [P, 512], U8)
 
         def block(k):
             return slice(k * P, (k + 1) * P)
 
-        def turned(name, b, shares):
-            g = work_tile("s_%s%d" % (name, b), [P, PACK * 512], BF16)
-            for engine, m0, m1 in shares:
-                cast_turned(engine, g, rows[name, b], m0, m1)
-            return g
+        def cast(engine, dst, src):
+            if engine == "v":
+                nc.vector.tensor_copy(out=dst, in_=src)
+            elif engine == "s":
+                nc.scalar.activation(out=dst, in_=src, func=COPY)
+            else:
+                nc.gpsimd.tensor_scalar(out=dst, in0=src, scalar1=1.0, scalar2=0.0, op0=MULT, op1=ADD)
 
-        def plain(name, b, engine, step=128):
-            g = work_tile("s_%s%d" % (name, b), [P, PACK * 512], BF16)
-            for c0 in range(0, 512, step):
-                cast_plain(engine, g[:, PACK * c0:PACK * (c0 + step)], rows[name, b], c0, c0 + step)
-            return g
+        gate = keep.tile([P, B, PACK], F32, name="gate")
+        gate2 = keep.tile([P, B, PACK], F32, name="gate2")
+        offsets = keep.tile([P, B * LIST_COLS], U16, name="offsets")
+        pool = [keep.tile([P, 2 * T], BF16, name="pool%d" % u) for u in range(2)]
 
-        def pair_cast(j0, j1, engine):
-            w = (j1 - j0) * P
-            g = work_tile("s_pair%d" % j0, [P, 2, PACK * w], BF16)
-            for k, name in enumerate(("dom", "qm")):
-                for j in range(j0, j1):
-                    cast_plain(engine, g[:, k, PACK * P * (j - j0):PACK * P * (j + 1 - j0)], rows[name, 0], j * P, (j + 1) * P)
-            return g
+        def window(j):
+            return tile("window%d" % j, [P, T], F32)
 
-        def pair_quant(j0, j1, g):
-            for k, name in enumerate(("dom", "qm")):
-                quant(name, 0, g[:, k, :], j0 * P, j1 * P)
+        def listed(b):
+            return offsets[:, b * LIST_COLS:(b + 1) * LIST_COLS]
 
-        def scores(b):
-            banks = []
-            for c in range(4):
-                bank = psum.tile([P, PACK, P], F32, name="a%d" % c, tag="a%d" % c)
-                for t in range(PACK):
-                    matmul(bank[:, t, :], ("q", b), block(t), ("c", b), block(c), True, True)
-                banks.append(bank)
-            return banks
+        def load_gate(e):
+            nc.sync.dma_start(out=gate[:], in_=rw.rearrange("b (p j) o -> p b (j o)", j=PACK))
+            nc.scalar.activation(out=gate2[:], in_=gate[:], func=COPY, scale=2.0)
 
-        def dscores(b):
-            banks = []
+        def load_list(e):
+            nc.sync.dma_start(offsets[:], offs)
+
+        def raw_pool(u, h):
+            return tile("r_c%d%d" % (u, h), [P, 2, H], F32)
+
+        def load_pool(e, u, h):
+            view = cT.rearrange("(p j) t -> p j t", j=PACK)
+            nc.sync.dma_start(out=raw_pool(u, h), in_=view[:, 2 * u:2 * u + 2, h * H:(h + 1) * H])
+
+        def raw(name, b):
+            return tile("r_%s%d" % (name, b), [P, PACK, 512], F32)
+
+        def load(e, name, b):
+            nc.sync.dma_start(out=raw(name, b), in_=source[name][b].rearrange("(p j) w -> p j w", j=PACK))
+
+        def zero(e, j):
+            (nc.vector if e == "v" else nc.gpsimd).memset(window(j), 0.0)
+
+        def cast_pool(e, u, h, c0, c1):
+            dst = pool[u][:, 2 * (h * H + c0):2 * (h * H + c1)].rearrange("p (c i e) -> p c e i", i=4, e=2)
+            cast(e, dst, raw_pool(u, h)[:, :, c0:c1].rearrange("p e (c i) -> p c e i", i=4))
+
+        def staged(name, b):
+            return tile("s_%s%d" % (name, b), [P, PACK * 512], BF16)
+
+        def gather(e, b, u):
+            if PLAIN[b]:
+                dst = tile("halves%d" % b, [P, (6 if HOST and b else 4) * N], BF16)[:, 2 * u * N:2 * (u + 1) * N].bitcast(U32)
+            else:
+                dst = staged("c", b).bitcast(U32)[:, u:2 * N:2]
+            nc.vector.tensor_copy(out=dst, in_=pool[u][:].bitcast(U32).indirect(listed(b)))
+
+        def weave(e, b):
+            src = tile("halves%d" % b, [P, (6 if HOST and b else 4) * N], BF16)[:, 0:4 * N]
+            dst = staged("c", b).rearrange("p (n u e) -> p n u e", u=2, e=2)
+            src = src.rearrange("p (u n e) -> p n u e", u=2, e=2)
+            if e == "s":
+                nc.scalar.copy(out=dst, in_=src)
+            else:
+                cast(e, dst, src)
+
+        def cast_turned(e, name, b, k):
+            ms = slice(32 * k, 32 * (k + 1))
+            cast(e, staged(name, b).rearrange("p (t m j) -> p m t j", t=PACK, j=PACK)[:, ms],
+                 raw(name, b).rearrange("p j (m t) -> p m t j", t=PACK)[:, ms])
+
+        def part(name, b, j0, j1):
+            return tile("s_%s%d_%d" % (name, b, j0), [P, PACK * P * (j1 - j0)], BF16)
+
+        def cast_plain(e, name, b, j0, j1, j):
+            dst = part(name, b, j0, j1)[:, PACK * P * (j - j0):PACK * P * (j + 1 - j0)]
+            cast(e, dst.rearrange("p (c i j) -> p c j i", i=4, j=PACK),
+                 raw(name, b)[:, :, block(j)].rearrange("p j (c i) -> p c j i", i=4))
+
+        def quant(e, name, b):
+            nc.vector.quantize_mx(out=codes(name, b).bitcast(FMT[name]), scales=scales(name, b), in_=staged(name, b))
+
+        def quant_part(e, name, b, j0, j1):
+            cols = slice(j0 * P, j1 * P)
+            nc.vector.quantize_mx(out=codes(name, b)[:, cols].bitcast(FMT[name]), scales=scales(name, b)[:, cols],
+                                  in_=part(name, b, j0, j1))
+
+        def matmul(dst, b, left, lcols, right, rcols, start, stop):
+            nc.tensor.matmul_mx(
+                out=dst,
+                lhsT=codes(left, b)[:, lcols].bitcast(FMT[left]), lhsT_scale=scales(left, b)[:, lcols],
+                rhs=codes(right, b)[:, rcols].bitcast(FMT[right]), rhs_scale=scales(right, b)[:, rcols],
+                start=start, stop=stop)
+
+        def a_bank(b, c):
+            return bank("a%d%d" % (b, c), [P, PACK, P])
+
+        def dp_bank(b, t):
+            return bank("dp%d%d" % (b, t), [P, N])
+
+        def grad_bank(b, j):
+            return bank("grad%d%d" % (b, j), [P, N])
+
+        def scores(e, b, c):
             for t in range(PACK):
-                bank = psum.tile([P, N], F32, name="dp%d" % t, tag="w%d" % DP_BANK[b][t])
-                matmul(bank[:], ("do", b), block(t), ("c", b), slice(0, N), True, True)
-                banks.append(bank)
-            return banks
+                matmul(a_bank(b, c)[:, t, :], b, "q", block(t), "c", block(c), True, True)
 
-        def gated_a(b, ga, a_banks, c):
+        def dscores(e, b, t):
+            matmul(dp_bank(b, t), b, "do", block(t), "c", slice(0, N), True, True)
+
+        def wide(name, b):
+            return tile("%s%d" % (name, b), [P, PACK * N], F32)
+
+        def by_t(name, b):
+            return wide(name, b).rearrange("p (t n) -> p t n", t=PACK)
+
+        def chunk(c):
+            return slice(c * PACK * P, (c + 1) * PACK * P)
+
+        def gated_a(e, b, c):
             for t in range(PACK):
-                nc.scalar.activation(out=ga[:, t, block(c)], in_=a_banks[c][:, t, :], func=COPY,
+                nc.scalar.activation(out=by_t("ga", b)[:, t, block(c)], in_=a_bank(b, c)[:, t, :], func=COPY,
                                      scale=gate[:, b, t:t + 1])
 
-        def gated_dp(b, gdp, dp_banks, t, engine):
-            if engine == "s":
-                nc.scalar.activation(out=gdp[:, t, :], in_=dp_banks[t][:], func=COPY, scale=gate2[:, b, t:t + 1])
+        def gated_dp(e, b, t):
+            if e == "s":
+                nc.scalar.activation(out=by_t("gdp", b)[:, t, :], in_=dp_bank(b, t), func=COPY,
+                                     scale=gate2[:, b, t:t + 1])
             else:
-                nc.vector.tensor_scalar(out=gdp[:, t, :], in0=dp_banks[t][:], scalar1=gate2[:, b, t:t + 1],
-                                        scalar2=None, op0=MULT)
+                nc.vector.tensor_scalar(out=by_t("gdp", b)[:, t, :], in0=dp_bank(b, t),
+                                        scalar1=gate2[:, b, t:t + 1], scalar2=None, op0=MULT)
 
-        def relu_times(dst, a_banks, other, c):
+        def relu_times(e, dst, other, b, c):
             nc.vector.scalar_tensor_tensor(
-                out=dst[:, PACK * c * P:PACK * (c + 1) * P].rearrange("p (n t) -> p n t", t=PACK),
-                in0=a_banks[c][:].rearrange("p t n -> p n t"), scalar=0.0,
-                in1=other[:, :, block(c)].rearrange("p t n -> p n t"),
+                out=staged(dst, b)[:, chunk(c)].rearrange("p (n t) -> p n t", t=PACK),
+                in0=a_bank(b, c).rearrange("p t n -> p n t"), scalar=0.0,
+                in1=by_t(other, b)[:, :, block(c)].rearrange("p t n -> p n t"),
                 op0=MAX, op1=MULT)
 
-        def gradients(b, js):
-            banks = {}
-            for j in js:
-                banks[j] = psum.tile([P, N], F32, name="grad%d%d" % (b, j), tag=GRAD_BANK[b][j])
-                matmul(banks[j][:], ("dom", b), block(j), ("pw", b), slice(0, N), True, False)
-            for j in js:
-                matmul(banks[j][:], ("qm", b), block(j), ("ds", b), slice(0, N), False, True)
-                grads[b, j] = work_tile("res%d%d" % (b, j), [P, N], F32)
-                nc.scalar.activation(out=grads[b, j][:], in_=banks[j][:], func=COPY)
+        def relu(e, b, c):
+            nc.scalar.activation(out=wide("ra", b)[:, chunk(c)].rearrange("p (n t) -> p n t", t=PACK),
+                                 in_=a_bank(b, c).rearrange("p t n -> p n t"), func=RELU)
 
-        def scatter(b, j):
-            nc.vector.tensor_copy(out=windows[j][:].indirect(offsets[:, b * LIST_COLS:(b + 1) * LIST_COLS]),
-                                  in_=grads[b, j][:])
+        def square(e, b, c):
+            nc.scalar.activation(out=wide("ga", b)[:, chunk(c)], in_=wide("ra", b)[:, chunk(c)], func=SQUARE)
 
-        grads = {}
-        quarters = [("s", 32 * k, 32 * (k + 1)) for k in range(4)]
-        picked0 = work_tile("picked0", [P, PACK * N], BF16)
-        cast_pool("s", 0, 0, 0, H)
-        cast_pool(C01, 0, 1, 0, H)
-        gather(0, 0, picked0[:].bitcast(U32)[:, 0:2 * N:2])
-        if LATE:
-            half0 = work_tile("half0", [P, 2 * N], BF16)
-            gather(1, 0, half0[:].bitcast(U32))
-        else:
-            picked1 = work_tile("picked1", [P, PACK * N], BF16)
-            gather(1, 0, picked1[:].bitcast(U32)[:, 0:2 * N:2])
-        cast_pool("s", 1, 0, 0, H)
-        if C11:
-            cast_pool("v", 1, 1, 0, C11)
-        cast_pool("s", 1, 1, C11, H)
-        for name, src in (("q", qT), ("do", doT), ("qm", qm), ("dom", dom)):
-            rows[name, 1] = load_rows("r_%s1" % name, src[1])
-        gather(0, 1, picked0[:].bitcast(U32)[:, 1:2 * N:2])
-        quant("c", 0, picked0[:])
-        if not LATE:
-            gather(1, 1, picked1[:].bitcast(U32)[:, 1:2 * N:2])
-            quant("c", 1, picked1[:])
+        def times_gate(e, b, k):
+            cols = slice(k * 2 * P, (k + 1) * 2 * P)
+            (nc.vector if e == "v" else nc.gpsimd).tensor_tensor(
+                out=staged("pw", b)[:, cols].rearrange("p (n t) -> p n t", t=PACK),
+                in0=wide("ga", b)[:, cols].rearrange("p (n t) -> p n t", t=PACK),
+                in1=gate[:, b, :].unsqueeze(1).to_broadcast([P, 2 * P // PACK, PACK]),
+                op=MULT)
 
-        quant("q", 0, turned("q", 0, [("s", 0, 64), ("s", 64, 128)])[:])
-        a_banks = scores(0)
-        quant("do", 0, turned("do", 0, [("s", 0, 64), (DO0B, 64, 128)])[:])
-        dp_banks = dscores(0)
-        ga = work_tile("ga0", [P, PACK, N], F32)
-        gdp = work_tile("gdp0", [P, PACK, N], F32)
-        pw = work_tile("pw0", [P, PACK * N], BF16)
-        ds = work_tile("ds0", [P, PACK * N], BF16)
-        for c in range(4):
-            gated_a(0, ga, a_banks, c)
-            relu_times(pw, a_banks, ga, c)
-        for t in range(PACK):
-            gated_dp(0, gdp, dp_banks, t, Y0[t])
-        quant("pw", 0, pw[:])
-        first = pair_cast(0, 2, "s")
-        for c in range(4):
-            relu_times(ds, a_banks, gdp, c)
-        pair_quant(0, 2, first)
-        quant("ds", 0, ds[:])
-        s_q1 = turned("q", 1, quarters)
-        if LATE:
-            half1 = work_tile("half1", [P, 2 * N], BF16)
-            gather(1, 1, half1[:].bitcast(U32))
-        gradients(0, [0, 1])
-        quant("q", 1, s_q1[:])
-        if LATE:
-            picked1 = work_tile("picked1", [P, PACK * N], BF16)
-            for u, half in enumerate((half0, half1)):
-                nc.scalar.copy(out=picked1[:].rearrange("p (n u e) -> p n u e", u=2, e=2)[:, :, u, :],
-                               in_=half[:].rearrange("p (n e) -> p n e", e=2))
-        scatter(0, 0)
-        if LATE:
-            quant("c", 1, picked1[:])
-        a_banks = scores(1)
-        pair_quant(2, 3, pair_cast(2, 3, "s"))
-        s_do1 = turned("do", 1, quarters)
-        scatter(0, 1)
-        gradients(0, [2])
-        quant("do", 1, s_do1[:])
-        dp_banks = dscores(1)
-        scatter(0, 2)
-        ga = work_tile("ga1", [P, PACK, N], F32)
-        gdp = work_tile("gdp1", [P, PACK, N], F32)
-        pw = work_tile("pw1", [P, PACK * N], BF16)
-        ds = work_tile("ds1", [P, PACK * N], BF16)
-        for c in range(4):
-            gated_a(1, ga, a_banks, c)
-            relu_times(pw, a_banks, ga, c)
-        for t in range(PACK):
-            gated_dp(1, gdp, dp_banks, t, "s")
-        quant("pw", 1, pw[:])
-        for c in range(4):
-            relu_times(ds, a_banks, gdp, c)
-        pair_quant(3, 4, pair_cast(3, 4, "s"))
-        quant("qm", 1, plain("qm", 1, "s")[:])
-        quant("dom", 1, plain("dom", 1, "s")[:])
-        quant("ds", 1, ds[:])
-        gradients(0, [3])
-        gradients(1, [0, 1, 2, 3])
-        scatter(0, 3)
+        def grad_dv(e, b, j):
+            matmul(grad_bank(b, j), b, "dom", block(j), "pw", slice(0, N), True, False)
+
+        def grad_dk(e, b, j):
+            matmul(grad_bank(b, j), b, "qm", block(j), "ds", slice(0, N), False, True)
+
+        def result(b, j):
+            return tile("res%d%d" % (b, j), [P, N], F32)
+
+        def leave(e, b, j):
+            cast(e, result(b, j), grad_bank(b, j))
+
+        def scatter(e, b, j):
+            nc.vector.tensor_copy(out=window(j).indirect(listed(b)), in_=result(b, j))
+
+        def store(e, j):
+            nc.sync.dma_start(out=out[block(j), :], in_=window(j))
+
+        def step(engines, fn, label, *args):
+            steps[label + "".join(str(a) for a in args)] = (engines, fn, args)
+
+        step("-", load_gate, "gate")
+        step("-", load_pool, "Lc", 0, 0)
+        step("-", load_list, "list")
+        step("-", load_pool, "Lc", 0, 1)
+        step("-", load_pool, "Lc", 1, 0)
+        step("-", load_pool, "Lc", 1, 1)
+        for name in ("q", "do", "dom", "qm"):
+            step("-", load, "L", name, 0)
         for j in range(4):
-            scatter(1, j)
-            nc.sync.dma_start(out=out[j * P:(j + 1) * P, :], in_=windows[j][:])
+            step("vg" if j < 2 else "gv", zero, "zero", j)
+        for h in range(2):
+            for c0 in (0, 512):
+                step("sv" if h == 0 else "vs", cast_pool, "P", 0, h, c0, c0 + 512)
+        step("-", gather, "G", 0, 0)
+        step("-", gather, "G", 1, 0)
+        for c0 in (0, 512):
+            step("sv", cast_pool, "P", 1, 0, c0, c0 + 512)
+        for c0 in (0, 256, 512, 768):
+            step("vs" if c0 < 512 else "sv", cast_pool, "P", 1, 1, c0, c0 + 256)
+        for name in ("q", "do", "dom", "qm"):
+            step("-", load, "L", name, 1)
+        for b in range(B):
+            step("-", gather, "G", b, 1)
+            if PLAIN[b]:
+                step("vsg", weave, "W", b)
+            step("-", quant, "Q", "c", b)
+            for name in ("q", "do"):
+                for k in range(4):
+                    step("svg", cast_turned, "T", name, b, k)
+                step("-", quant, "Q", name, b)
+            for c in range(4):
+                step("-", scores, "A", b, c)
+            for t in range(PACK):
+                step("-", dscores, "D", b, t)
+            for c in range(4):
+                if SQ[b]:
+                    step("-", relu, "R", b, c)
+                    step("-", square, "S", b, c)
+                    step("gv", times_gate, "M", b, 2 * c)
+                    step("gv", times_gate, "M", b, 2 * c + 1)
+                else:
+                    step("-", gated_a, "X", b, c)
+                    step("-", relu_times, "E", "pw", "ga", b, c)
+            for t in range(PACK):
+                step("sv", gated_dp, "Y", b, t)
+            step("-", quant, "Q", "pw", b)
+            for c in range(4):
+                step("-", relu_times, "E", "ds", "gdp", b, c)
+            step("-", quant, "Q", "ds", b)
+            for j0, j1 in GROUPS[b]:
+                for name in ("dom", "qm"):
+                    for j in range(j0, j1):
+                        step("svg", cast_plain, "C", name, b, j0, j1, j)
+                    step("-", quant_part, "Q", name, b, j0, j1)
+                for j in range(j0, j1):
+                    step("-", grad_dv, "V", b, j)
+                    step("-", grad_dk, "K", b, j)
+                    step("sv", leave, "O", b, j)
+                    step("-", scatter, "Z", b, j)
+        for j in range(4):
+            step("-", store, "St", j)
+
+        for label in ORDER or list(steps):
+            engines, fn, args = steps[label]
+            fn(ENG.get(label, engines[0]), *args)

@@ -24,13 +24,14 @@ PACK = 4
 LIST_COLS = N // 16
 H = T // 2
 FMT = {"c": E4M3, "q": E4M3, "do": E5M2, "qm": E4M3, "dom": E5M2, "pw": E4M3, "ds": E5M2}
-GROUPS = [[(0, 2), (2, 3), (3, 4)], [(0, 4)]]
 HOST = "s_ds0"
 PLAIN = [False, True]
 SQ = [False, True]
-TAG = {"res03": "ga1", "s_qm1_0": "x_c1", "r_dom1": "e_q1", "grad11": "dp13", "gdp1": "x_do0", "a12": "dp02", "window1": "r_do0", "grad12": "a03", "s_pw0": "r_do0", "s_pw1": "x_do1", "a11": "a00", "grad10": "a03", "r_dom0": "r_c00", "gdp0": "r_q0", "s_do1": "x_q0", "ra1": "r_q0", "s_dom0_2": "r_do1", "s_dom1_0": "r_qm0", "res10": "x_qm1", "a13": "a03", "s_q1": "x_do0", "grad02": "a01", "grad03": "a00", "grad01": "a00", "dp11": "dp02", "grad13": "a01", "dp10": "dp00", "dp01": "dp02", "r_q1": "e_c0", "s_q0": "r_c01", "a10": "dp03", "res01": "r_c00", "dp12": "dp00", "grad00": "a01"}
-ENG = {"zero0": "v", "zero1": "g", "zero2": "g", "zero3": "g", "P000512": "v", "P005121024": "v", "P010512": "s", "P015121024": "v", "P100512": "s", "P105121024": "s", "P110256": "v", "P11256512": "v", "P11512768": "s", "P117681024": "v", "W1": "s", "Tq00": "v", "Tq01": "s", "Tq02": "s", "Tq03": "g", "Tdo00": "s", "Tdo01": "v", "Tdo02": "v", "Tdo03": "v", "Y00": "s", "Y01": "s", "Y02": "s", "Y03": "s", "Cdom0020": "s", "Cdom0021": "s", "Cqm0020": "g", "Cqm0021": "g", "O00": "v", "O01": "s", "Tq10": "s", "Tq11": "s", "Tq12": "s", "Tq13": "s", "Tdo10": "s", "Tdo11": "s", "Tdo12": "s", "Tdo13": "g", "Cdom0232": "s", "Cqm0232": "s", "Y10": "s", "Y11": "s", "Y12": "s", "Y13": "v", "O02": "s", "M10": "g", "M11": "g", "M12": "g", "M13": "g", "M14": "g", "M15": "g", "M16": "g", "M17": "g", "Cdom0343": "s", "Cqm0343": "s", "Cdom1040": "s", "Cdom1041": "s", "Cdom1042": "s", "Cdom1043": "s", "Cqm1040": "s", "Cqm1041": "s", "Cqm1042": "g", "Cqm1043": "s", "O03": "s", "O10": "s", "O11": "s", "O12": "s", "O13": "s"}
-ORDER = ["Lc00", "zero3", "Lc01", "list", "Lc10", "P100512", "Lc11", "gate", "P015121024", "P11256512", "P010512", "Lq0", "Tq01", "P000512", "P117681024", "Tq00", "Ldo0", "P105121024", "Tdo00", "P005121024", "Tq02", "P110256", "P11512768", "G01", "Tdo01", "Tq03", "Qq0", "G00", "Qc0", "A03", "Tdo02", "Tdo03", "X03", "Qdo0", "A01", "A00", "Ldo1", "Ldom0", "X01", "X00", "A02", "D02", "Cdom0021", "Epwga00", "Epwga03", "Y02", "Epwga01", "D01", "X02", "Y01", "D00", "Y00", "D03", "Epwga02", "Y03", "Lq1", "zero0", "Tdo11", "Edsgdp00", "Edsgdp01", "zero2", "Qpw0", "Tq13", "Tq11", "Tq10", "Edsgdp02", "Lqm0", "Cdom0020", "Cqm0021", "Tdo12", "Edsgdp03", "Tdo10", "Cqm0020", "Qds0", "Qqm002", "Tq12", "G10", "G11", "Tdo13", "Qdom002", "Qq1", "V00", "K00", "Cdom0232", "W1", "Qc1", "Qdo1", "V01", "K01", "D10", "D11", "Cdom0343", "Y10", "O01", "Y11", "A13", "A10", "Cqm0232", "A11", "D12", "R13", "D13", "R11", "O00", "Qdom023", "zero1", "Cqm0343", "R10", "Z01", "Y12", "S10", "V02", "Z00", "Y13", "A12", "Qqm023", "K02", "Ldom1", "Lqm1", "R12", "Cdom1043", "Cdom1041", "Edsgdp10", "Qdom034", "S12", "M14", "M11", "Edsgdp11", "Edsgdp12", "Edsgdp13", "S11", "V03", "S13", "Cdom1042", "M10", "M15", "O02", "M13", "Qqm034", "Qds1", "M17", "M12", "Cqm1042", "Z02", "M16", "K03", "Cqm1043", "Qpw1", "Cdom1040", "Cqm1041", "Qdom104", "V11", "Cqm1040", "V12", "Qqm104", "K12", "O03", "V13", "O12", "V10", "K11", "K10", "K13", "O11", "Z11", "St1", "Z03", "O10", "O13", "Z13", "Z12", "St3", "Z10", "St0", "St2"]
+DSG = [[], [3]]
+GROUPS = [[(0, 2), (2, 4)], [(0, 4)]]
+TAG = {"grad03": "dp02", "dp10": "a01", "grad02": "a01", "grad00": "a00", "a10": "dp00", "a11": "a02", "grad10": "a02", "grad13": "dp00", "grad11": "a01", "grad12": "a03", "dp13": "a00", "grad01": "dp00", "a12": "a03", "a13": "dp03", "dp12": "dp03", "dp11": "dp02", "x_q1": "pool1", "s_qm0_2": "r_dom0", "s_ds1": "x_pw0", "res13": "res02", "s_dom1_0": "e_pw0", "s_qm1_0": "e_ds0", "x_qm1": "x_qm0", "r_dom1": "r_do0", "x_ds1": "x_ds0", "s_pw0": "r_do0", "gdp1": "r_qm0", "x_dom0": "x_c0", "ga1": "r_do1", "r_qm1": "r_dom0", "gdp0": "s_c0", "s_q0": "r_c01", "res00": "s_q1"}
+ENG = {"zero0": "v", "zero1": "g", "zero2": "v", "zero3": "v", "P000512": "s", "P005121024": "s", "P010512": "s", "P015121024": "v", "P100512": "v", "P105121024": "s", "P110256": "v", "P11256512": "s", "P11512768": "v", "P117681024": "s", "Tq00": "v", "Tq01": "s", "Tq02": "g", "Tq03": "s", "Tdo00": "s", "Tdo01": "v", "Tdo02": "v", "Tdo03": "v", "Y00": "s", "Y01": "s", "Y02": "s", "Y03": "v", "Cdom0020": "g", "Cdom0021": "g", "Cqm0020": "s", "Cqm0021": "s", "O00": "s", "O01": "s", "Cdom0242": "s", "Cdom0243": "g", "Cqm0242": "s", "Cqm0243": "s", "O02": "s", "O03": "s", "W1": "s", "Tq10": "g", "Tq11": "g", "Tq12": "s", "Tq13": "s", "Tdo10": "s", "Tdo11": "v", "Tdo12": "s", "Tdo13": "g", "M10": "g", "M11": "g", "M12": "g", "M13": "g", "M14": "g", "M15": "g", "M16": "g", "M17": "g", "Y10": "s", "Y11": "s", "Y12": "s", "Y13": "s", "N16": "g", "N17": "g", "Cdom1040": "s", "Cdom1041": "s", "Cdom1042": "s", "Cdom1043": "s", "Cqm1040": "s", "Cqm1041": "s", "Cqm1042": "s", "Cqm1043": "s", "O10": "s", "O11": "s", "O12": "s", "O13": "s"}
+ORDER = ["Lc00","list","Lc01","Lc10","zero0","zero1","zero2","zero3","P000512","P005121024","Lc11","Lq0","Ldo0","gate","P100512","P105121024","P110256","P11256512","P11512768","P117681024","Ldom0","P010512","P015121024","G00","G10","Lq1","Ldo1","G01","Qc0","Tq00","Tq01","Tq02","Tq03","Qq0","Tdo00","Tdo01","Tdo02","Tdo03","Qdo0","Cdom0020","Cdom0021","Lqm0","A01","D00","X01","Epwga01","A00","Tq10","Tq11","A02","A03","D03","X00","Epwga00","Y03","D01","D02","X03","Epwga03","X02","Epwga02","Y00","Y01","Y02","Cdom0242","Cdom0243","Edsgdp00","Edsgdp01","Edsgdp02","Edsgdp03","Qds0","Qdom002","Cqm0020","Cqm0021","Qpw0","Cqm0242","Cqm0243","Qqm024","Tq12","Tq13","Tdo11","Tdo12","Tdo13","G11","W1","Qc1","Qq1","Tdo10","A13","Qqm002","V00","R13","S13","V01","K01","O01","Z01","Qdo1","A10","Qdom024","K00","O00","Z00","D13","R10","S10","M10","M11","A11","A12","Ldom1","Lqm1","V02","K02","O02","Z02","D10","D11","D12","R11","S11","M12","M13","R12","Y12","Y13","Y11","V03","K03","Cqm1040","Cqm1041","Cqm1042","Cqm1043","Qqm104","Y10","S12","M14","M15","Edsgdp10","Edsgdp11","Edsgdp12","M16","M17","N16","N17","Qds1","Cdom1040","Cdom1041","Cdom1042","Cdom1043","Qdom104","Qpw1","V10","K10","V12","K12","O03","Z03","V13","K13","O10","Z10","St0","V11","O12","Z12","St2","O13","Z13","St3","K11","O11","Z11","St1"]
 
 
 def tile_attend_gat_c_kernel(tc, qT, cT, doT, rw, qm, dom, offs, out):
@@ -76,10 +77,12 @@ def tile_attend_gat_c_kernel(tc, qT, cT, doT, rw, qm, dom, offs, out):
         gate = keep.tile([P, B, PACK], F32, name="gate")
         gate2 = keep.tile([P, B, PACK], F32, name="gate2")
         offsets = keep.tile([P, B * LIST_COLS], U16, name="offsets")
-        pool = [keep.tile([P, 2 * T], BF16, name="pool%d" % u) for u in range(2)]
 
         def window(j):
             return tile("window%d" % j, [P, T], F32)
+
+        def pairs(u):
+            return tile("pool%d" % u, [P, 2 * T], BF16)
 
         def listed(b):
             return offsets[:, b * LIST_COLS:(b + 1) * LIST_COLS]
@@ -108,7 +111,7 @@ def tile_attend_gat_c_kernel(tc, qT, cT, doT, rw, qm, dom, offs, out):
             (nc.vector if e == "v" else nc.gpsimd).memset(window(j), 0.0)
 
         def cast_pool(e, u, h, c0, c1):
-            dst = pool[u][:, 2 * (h * H + c0):2 * (h * H + c1)].rearrange("p (c i e) -> p c e i", i=4, e=2)
+            dst = pairs(u)[:, 2 * (h * H + c0):2 * (h * H + c1)].rearrange("p (c i e) -> p c e i", i=4, e=2)
             cast(e, dst, raw_pool(u, h)[:, :, c0:c1].rearrange("p e (c i) -> p c e i", i=4))
 
         def staged(name, b):
@@ -119,7 +122,7 @@ def tile_attend_gat_c_kernel(tc, qT, cT, doT, rw, qm, dom, offs, out):
                 dst = tile("halves%d" % b, [P, (6 if HOST and b else 4) * N], BF16)[:, 2 * u * N:2 * (u + 1) * N].bitcast(U32)
             else:
                 dst = staged("c", b).bitcast(U32)[:, u:2 * N:2]
-            nc.vector.tensor_copy(out=dst, in_=pool[u][:].bitcast(U32).indirect(listed(b)))
+            nc.vector.tensor_copy(out=dst, in_=pairs(u).bitcast(U32).indirect(listed(b)))
 
         def weave(e, b):
             src = tile("halves%d" % b, [P, (6 if HOST and b else 4) * N], BF16)[:, 0:4 * N]
@@ -218,6 +221,14 @@ def tile_attend_gat_c_kernel(tc, qT, cT, doT, rw, qm, dom, offs, out):
                 in1=gate[:, b, :].unsqueeze(1).to_broadcast([P, 2 * P // PACK, PACK]),
                 op=MULT)
 
+        def relu_product(e, b, k):
+            cols = slice(k * 2 * P, (k + 1) * 2 * P)
+            (nc.vector if e == "v" else nc.gpsimd).tensor_tensor(
+                out=staged("ds", b)[:, cols].rearrange("p (n t) -> p n t", t=PACK),
+                in0=wide("ra", b)[:, cols].rearrange("p (n t) -> p n t", t=PACK),
+                in1=by_t("gdp", b)[:, :, k * P // 2:(k + 1) * P // 2].rearrange("p t n -> p n t"),
+                op=MULT)
+
         def grad_dv(e, b, j):
             matmul(grad_bank(b, j), b, "dom", block(j), "pw", slice(0, N), True, False)
 
@@ -286,7 +297,11 @@ def tile_attend_gat_c_kernel(tc, qT, cT, doT, rw, qm, dom, offs, out):
                 step("sv", gated_dp, "Y", b, t)
             step("-", quant, "Q", "pw", b)
             for c in range(4):
-                step("-", relu_times, "E", "ds", "gdp", b, c)
+                if c in DSG[b]:
+                    step("gv", relu_product, "N", b, 2 * c)
+                    step("gv", relu_product, "N", b, 2 * c + 1)
+                else:
+                    step("-", relu_times, "E", "ds", "gdp", b, c)
             step("-", quant, "Q", "ds", b)
             for j0, j1 in GROUPS[b]:
                 for name in ("dom", "qm"):

@@ -19,19 +19,44 @@ MULT = mybir.AluOpType.mult
 ADD = mybir.AluOpType.add
 MAX = mybir.AluOpType.max
 
+VECTOR, SCALAR, GPSIMD = "vector", "scalar", "gpsimd"
+
 P = 128
 PACK = 4
+WIDTH = 512
 LIST_COLS = N // 16
-H = T // 2
-FMT = {"c": E4M3, "q": E4M3, "do": E5M2, "qm": E4M3, "dom": E5M2, "pw": E4M3, "ds": E5M2}
-HOST = "s_ds0"
-PLAIN = [False, True]
-SQ = [False, True]
-DSG = [[], [3]]
-GROUPS = [[(0, 2), (2, 4)], [(0, 4)]]
-TAG = {"grad03": "dp02", "dp10": "a01", "grad02": "a01", "grad00": "a00", "a10": "dp00", "a11": "a02", "grad10": "a02", "grad13": "dp00", "grad11": "a01", "grad12": "a03", "dp13": "a00", "grad01": "dp00", "a12": "a03", "a13": "dp03", "dp12": "dp03", "dp11": "dp02", "x_q1": "pool1", "s_qm0_2": "r_dom0", "s_ds1": "x_pw0", "res13": "res02", "s_dom1_0": "e_pw0", "s_qm1_0": "e_ds0", "x_qm1": "x_qm0", "r_dom1": "r_do0", "x_ds1": "x_ds0", "s_pw0": "r_do0", "gdp1": "r_qm0", "x_dom0": "x_c0", "ga1": "r_do1", "r_qm1": "r_dom0", "gdp0": "s_c0", "s_q0": "r_c01", "res00": "s_q1"}
-ENG = {"zero0": "v", "zero1": "g", "zero2": "v", "zero3": "v", "P000512": "s", "P005121024": "s", "P010512": "s", "P015121024": "v", "P100512": "v", "P105121024": "s", "P110256": "v", "P11256512": "s", "P11512768": "v", "P117681024": "s", "Tq00": "v", "Tq01": "s", "Tq02": "g", "Tq03": "s", "Tdo00": "s", "Tdo01": "v", "Tdo02": "v", "Tdo03": "v", "Y00": "s", "Y01": "s", "Y02": "s", "Y03": "v", "Cdom0020": "g", "Cdom0021": "g", "Cqm0020": "s", "Cqm0021": "s", "O00": "s", "O01": "s", "Cdom0242": "s", "Cdom0243": "g", "Cqm0242": "s", "Cqm0243": "s", "O02": "s", "O03": "s", "W1": "s", "Tq10": "g", "Tq11": "g", "Tq12": "s", "Tq13": "s", "Tdo10": "s", "Tdo11": "v", "Tdo12": "s", "Tdo13": "g", "M10": "g", "M11": "g", "M12": "g", "M13": "g", "M14": "g", "M15": "g", "M16": "g", "M17": "g", "Y10": "s", "Y11": "s", "Y12": "s", "Y13": "s", "N16": "g", "N17": "g", "Cdom1040": "s", "Cdom1041": "s", "Cdom1042": "s", "Cdom1043": "s", "Cqm1040": "s", "Cqm1041": "s", "Cqm1042": "s", "Cqm1043": "s", "O10": "s", "O11": "s", "O12": "s", "O13": "s"}
-ORDER = ["Lc00","list","Lc01","Lc10","zero0","zero1","zero2","zero3","P000512","P005121024","Lc11","Lq0","Ldo0","gate","P100512","P105121024","P110256","P11256512","P11512768","P117681024","Ldom0","P010512","P015121024","G00","G10","Lq1","Ldo1","G01","Qc0","Tq00","Tq01","Tq02","Tq03","Qq0","Tdo00","Tdo01","Tdo02","Tdo03","Qdo0","Cdom0020","Cdom0021","Lqm0","A01","D00","X01","Epwga01","A00","Tq10","Tq11","A02","A03","D03","X00","Epwga00","Y03","D01","D02","X03","Epwga03","X02","Epwga02","Y00","Y01","Y02","Cdom0242","Cdom0243","Edsgdp00","Edsgdp01","Edsgdp02","Edsgdp03","Qds0","Qdom002","Cqm0020","Cqm0021","Qpw0","Cqm0242","Cqm0243","Qqm024","Tq12","Tq13","Tdo11","Tdo12","Tdo13","G11","W1","Qc1","Qq1","Tdo10","A13","Qqm002","V00","R13","S13","V01","K01","O01","Z01","Qdo1","A10","Qdom024","K00","O00","Z00","D13","R10","S10","M10","M11","A11","A12","Ldom1","Lqm1","V02","K02","O02","Z02","D10","D11","D12","R11","S11","M12","M13","R12","Y12","Y13","Y11","V03","K03","Cqm1040","Cqm1041","Cqm1042","Cqm1043","Qqm104","Y10","S12","M14","M15","Edsgdp10","Edsgdp11","Edsgdp12","M16","M17","N16","N17","Qds1","Cdom1040","Cdom1041","Cdom1042","Cdom1043","Qdom104","Qpw1","V10","K10","V12","K12","O03","Z03","V13","K13","O10","Z10","St0","V11","O12","Z12","St2","O13","Z13","St3","K11","O11","Z11","St1"]
+HALF = T // 2
+LINE = 4
+TURN = 32
+GATE_STEP = 256
+FORMAT = {"c": E4M3, "q": E4M3, "do": E5M2, "qm": E4M3, "dom": E5M2, "pw": E4M3, "ds": E5M2}
+
+SBUF_TURNS = [
+    ["raw_c00", "bf_q0"],
+    ["raw_c01", "halves"],
+    ["raw_c10", "gated_dp0"],
+    ["pairs1", "bf_c1"],
+    ["raw_q0", "raw_dom1"],
+    ["raw_do0", "bf_dom0_2"],
+    ["raw_q1", "codes_do1"],
+    ["bf_do0", "raw_do1", "relu_a", "bf_qm1_0"],
+    ["bf_dom0_0", "bf_qm0_2"],
+    ["bf_dom1_0", "codes_ds1"],
+    ["codes_dom0", "grad_sb03"],
+    ["codes_c1", "codes_dom1"],
+    ["codes_pw0", "raw_qm1"],
+    ["squares", "codes_qm1"],
+]
+PSUM_TURNS = [
+    ["dp00", "dp10", "a11", "grad13", "grad11"],
+    ["dp01", "dp02", "a12"],
+    ["dp03", "a10"],
+    ["a00", "grad03", "dp13", "dp12"],
+    ["a01", "a13"],
+    ["a02", "grad01", "dp11", "grad12", "grad10"],
+    ["a03", "grad02"],
+]
+BUFFER = {name: turns[0] for turns in SBUF_TURNS + PSUM_TURNS for name in turns}
 
 
 def tile_attend_gat_c_kernel(tc, qT, cT, doT, rw, qm, dom, offs, out):
@@ -43,123 +68,53 @@ def tile_attend_gat_c_kernel(tc, qT, cT, doT, rw, qm, dom, offs, out):
         work = ctx.enter_context(tc.tile_pool(name="work", bufs=1))
         psum = ctx.enter_context(tc.psum_pool(name="psum", bufs=1))
         tiles = {}
-        steps = {}
+
 
         def tile(name, shape, dtype):
-            if name == HOST:
-                return tile("halves1", [P, 6 * N], BF16)[:, 2 * N:6 * N]
             if name not in tiles:
-                tiles[name] = work.tile(shape, dtype, name=name, tag=TAG.get(name, name), align_bytes=64)
+                tiles[name] = work.tile(shape, dtype, name=name, tag=BUFFER.get(name, name), align_bytes=64)
             return tiles[name][:]
 
         def bank(name, shape):
             if name not in tiles:
-                tiles[name] = psum.tile(shape, F32, name=name, tag=TAG.get(name, name))
+                tiles[name] = psum.tile(shape, F32, name=name, tag=BUFFER.get(name, name))
             return tiles[name][:]
-
-        def codes(name, b):
-            return tile("x_%s%d" % (name, b), [P, 512], U32)
-
-        def scales(name, b):
-            return tile("e_%s%d" % (name, b), [P, 512], U8)
-
-        def block(k):
-            return slice(k * P, (k + 1) * P)
-
-        def cast(engine, dst, src):
-            if engine == "v":
-                nc.vector.tensor_copy(out=dst, in_=src)
-            elif engine == "s":
-                nc.scalar.activation(out=dst, in_=src, func=COPY)
-            else:
-                nc.gpsimd.tensor_scalar(out=dst, in0=src, scalar1=1.0, scalar2=0.0, op0=MULT, op1=ADD)
 
         gate = keep.tile([P, B, PACK], F32, name="gate")
         gate2 = keep.tile([P, B, PACK], F32, name="gate2")
         offsets = keep.tile([P, B * LIST_COLS], U16, name="offsets")
 
-        def window(j):
-            return tile("window%d" % j, [P, T], F32)
-
-        def pairs(u):
-            return tile("pool%d" % u, [P, 2 * T], BF16)
-
         def listed(b):
             return offsets[:, b * LIST_COLS:(b + 1) * LIST_COLS]
 
-        def load_gate(e):
-            nc.sync.dma_start(out=gate[:], in_=rw.rearrange("b (p j) o -> p b (j o)", j=PACK))
-            nc.scalar.activation(out=gate2[:], in_=gate[:], func=COPY, scale=2.0)
-
-        def load_list(e):
-            nc.sync.dma_start(offsets[:], offs)
+        def block(i):
+            return slice(i * P, (i + 1) * P)
 
         def raw_pool(u, h):
-            return tile("r_c%d%d" % (u, h), [P, 2, H], F32)
+            return tile("raw_c%d%d" % (u, h), [P, 2, HALF], F32)
 
-        def load_pool(e, u, h):
-            view = cT.rearrange("(p j) t -> p j t", j=PACK)
-            nc.sync.dma_start(out=raw_pool(u, h), in_=view[:, 2 * u:2 * u + 2, h * H:(h + 1) * H])
+        def pairs(u):
+            return tile("pairs%d" % u, [P, 2 * T], BF16)
+
+        def halves():
+            return tile("halves", [P, 6 * N], BF16)
 
         def raw(name, b):
-            return tile("r_%s%d" % (name, b), [P, PACK, 512], F32)
-
-        def load(e, name, b):
-            nc.sync.dma_start(out=raw(name, b), in_=source[name][b].rearrange("(p j) w -> p j w", j=PACK))
-
-        def zero(e, j):
-            (nc.vector if e == "v" else nc.gpsimd).memset(window(j), 0.0)
-
-        def cast_pool(e, u, h, c0, c1):
-            dst = pairs(u)[:, 2 * (h * H + c0):2 * (h * H + c1)].rearrange("p (c i e) -> p c e i", i=4, e=2)
-            cast(e, dst, raw_pool(u, h)[:, :, c0:c1].rearrange("p e (c i) -> p c e i", i=4))
+            return tile("raw_%s%d" % (name, b), [P, PACK, WIDTH], F32)
 
         def staged(name, b):
-            return tile("s_%s%d" % (name, b), [P, PACK * 512], BF16)
+            if (name, b) == ("pw", 0):
+                return halves()[:, 2 * N:6 * N]
+            return tile("bf_%s%d" % (name, b), [P, PACK * WIDTH], BF16)
 
-        def gather(e, b, u):
-            if PLAIN[b]:
-                dst = tile("halves%d" % b, [P, (6 if HOST and b else 4) * N], BF16)[:, 2 * u * N:2 * (u + 1) * N].bitcast(U32)
-            else:
-                dst = staged("c", b).bitcast(U32)[:, u:2 * N:2]
-            nc.vector.tensor_copy(out=dst, in_=pairs(u).bitcast(U32).indirect(listed(b)))
+        def staged_part(name, b, j0, j1):
+            return tile("bf_%s%d_%d" % (name, b, j0), [P, PACK * P * (j1 - j0)], BF16)
 
-        def weave(e, b):
-            src = tile("halves%d" % b, [P, (6 if HOST and b else 4) * N], BF16)[:, 0:4 * N]
-            dst = staged("c", b).rearrange("p (n u e) -> p n u e", u=2, e=2)
-            src = src.rearrange("p (u n e) -> p n u e", u=2, e=2)
-            if e == "s":
-                nc.scalar.copy(out=dst, in_=src)
-            else:
-                cast(e, dst, src)
+        def codes(name, b):
+            return tile("codes_%s%d" % (name, b), [P, WIDTH], U32)
 
-        def cast_turned(e, name, b, k):
-            ms = slice(32 * k, 32 * (k + 1))
-            cast(e, staged(name, b).rearrange("p (t m j) -> p m t j", t=PACK, j=PACK)[:, ms],
-                 raw(name, b).rearrange("p j (m t) -> p m t j", t=PACK)[:, ms])
-
-        def part(name, b, j0, j1):
-            return tile("s_%s%d_%d" % (name, b, j0), [P, PACK * P * (j1 - j0)], BF16)
-
-        def cast_plain(e, name, b, j0, j1, j):
-            dst = part(name, b, j0, j1)[:, PACK * P * (j - j0):PACK * P * (j + 1 - j0)]
-            cast(e, dst.rearrange("p (c i j) -> p c j i", i=4, j=PACK),
-                 raw(name, b)[:, :, block(j)].rearrange("p j (c i) -> p c j i", i=4))
-
-        def quant(e, name, b):
-            nc.vector.quantize_mx(out=codes(name, b).bitcast(FMT[name]), scales=scales(name, b), in_=staged(name, b))
-
-        def quant_part(e, name, b, j0, j1):
-            cols = slice(j0 * P, j1 * P)
-            nc.vector.quantize_mx(out=codes(name, b)[:, cols].bitcast(FMT[name]), scales=scales(name, b)[:, cols],
-                                  in_=part(name, b, j0, j1))
-
-        def matmul(dst, b, left, lcols, right, rcols, start, stop):
-            nc.tensor.matmul_mx(
-                out=dst,
-                lhsT=codes(left, b)[:, lcols].bitcast(FMT[left]), lhsT_scale=scales(left, b)[:, lcols],
-                rhs=codes(right, b)[:, rcols].bitcast(FMT[right]), rhs_scale=scales(right, b)[:, rcols],
-                start=start, stop=stop)
+        def scales(name, b):
+            return tile("scales_%s%d" % (name, b), [P, WIDTH], U8)
 
         def a_bank(b, c):
             return bank("a%d%d" % (b, c), [P, PACK, P])
@@ -170,152 +125,293 @@ def tile_attend_gat_c_kernel(tc, qT, cT, doT, rw, qm, dom, offs, out):
         def grad_bank(b, j):
             return bank("grad%d%d" % (b, j), [P, N])
 
-        def scores(e, b, c):
-            for t in range(PACK):
-                matmul(a_bank(b, c)[:, t, :], b, "q", block(t), "c", block(c), True, True)
+        def wide(name):
+            return tile(name, [P, PACK * N], F32)
 
-        def dscores(e, b, t):
-            matmul(dp_bank(b, t), b, "do", block(t), "c", slice(0, N), True, True)
-
-        def wide(name, b):
-            return tile("%s%d" % (name, b), [P, PACK * N], F32)
-
-        def by_t(name, b):
-            return wide(name, b).rearrange("p (t n) -> p t n", t=PACK)
+        def by_t(name):
+            return wide(name).rearrange("p (t n) -> p t n", t=PACK)
 
         def chunk(c):
             return slice(c * PACK * P, (c + 1) * PACK * P)
 
-        def gated_a(e, b, c):
-            for t in range(PACK):
-                nc.scalar.activation(out=by_t("ga", b)[:, t, block(c)], in_=a_bank(b, c)[:, t, :], func=COPY,
-                                     scale=gate[:, b, t:t + 1])
+        def grad_sbuf(b, j):
+            return tile("grad_sb%d%d" % (b, j), [P, N], F32)
 
-        def gated_dp(e, b, t):
-            if e == "s":
-                nc.scalar.activation(out=by_t("gdp", b)[:, t, :], in_=dp_bank(b, t), func=COPY,
-                                     scale=gate2[:, b, t:t + 1])
+        def window(j):
+            return tile("window%d" % j, [P, T], F32)
+
+
+        def load_gate():
+            nc.sync.dma_start(out=gate[:], in_=rw.rearrange("b (p j) o -> p b (j o)", j=PACK))
+            nc.scalar.activation(out=gate2[:], in_=gate[:], func=COPY, scale=2.0)
+
+        def load_list():
+            nc.sync.dma_start(offsets[:], offs)
+
+        def load_pool(u, h):
+            view = cT.rearrange("(p j) t -> p j t", j=PACK)
+            nc.sync.dma_start(out=raw_pool(u, h), in_=view[:, 2 * u:2 * u + 2, h * HALF:(h + 1) * HALF])
+
+        def load(name, b):
+            nc.sync.dma_start(out=raw(name, b), in_=source[name][b].rearrange("(p j) w -> p j w", j=PACK))
+
+        def store(j):
+            nc.sync.dma_start(out=out[block(j), :], in_=window(j))
+
+
+        def cast(engine, dst, src):
+            if engine == VECTOR:
+                nc.vector.tensor_copy(out=dst, in_=src)
+            elif engine == SCALAR:
+                nc.scalar.activation(out=dst, in_=src, func=COPY)
             else:
-                nc.vector.tensor_scalar(out=by_t("gdp", b)[:, t, :], in0=dp_bank(b, t),
-                                        scalar1=gate2[:, b, t:t + 1], scalar2=None, op0=MULT)
+                nc.gpsimd.tensor_scalar(out=dst, in0=src, scalar1=1.0, scalar2=0.0, op0=MULT, op1=ADD)
 
-        def relu_times(e, dst, other, b, c):
+        def cast_pool(engine, u, h, c0, c1):
+            first = h * HALF
+            dst = pairs(u)[:, 2 * (first + c0):2 * (first + c1)].rearrange("p (c i e) -> p c e i", i=LINE, e=2)
+            cast(engine, dst, raw_pool(u, h)[:, :, c0:c1].rearrange("p e (c i) -> p c e i", i=LINE))
+
+        def cast_turned(engine, name, b, quarter):
+            ms = slice(TURN * quarter, TURN * (quarter + 1))
+            cast(engine, staged(name, b).rearrange("p (t m j) -> p m t j", t=PACK, j=PACK)[:, ms],
+                 raw(name, b).rearrange("p j (m t) -> p m t j", t=PACK)[:, ms])
+
+        def cast_plain(engine, name, b, j0, j1, j):
+            dst = staged_part(name, b, j0, j1)[:, PACK * P * (j - j0):PACK * P * (j + 1 - j0)]
+            cast(engine, dst.rearrange("p (c i j) -> p c j i", i=LINE, j=PACK),
+                 raw(name, b)[:, :, block(j)].rearrange("p j (c i) -> p c j i", i=LINE))
+
+
+        def gather(b, u, dst):
+            nc.vector.tensor_copy(out=dst, in_=pairs(u).bitcast(U32).indirect(listed(b)))
+
+        def gather_woven(u):
+            gather(0, u, staged("c", 0).bitcast(U32)[:, u:2 * N:2])
+
+        def gather_half(u):
+            gather(1, u, halves()[:, 2 * u * N:2 * (u + 1) * N].bitcast(U32))
+
+        def weave_halves():
+            nc.scalar.copy(out=staged("c", 1).rearrange("p (n u e) -> p n u e", u=2, e=2),
+                           in_=halves()[:, 0:4 * N].rearrange("p (u n e) -> p n u e", u=2, e=2))
+
+        def zero(engine, j):
+            (nc.vector if engine == VECTOR else nc.gpsimd).memset(window(j), 0.0)
+
+        def scatter(b, j):
+            nc.vector.tensor_copy(out=window(j).indirect(listed(b)), in_=grad_sbuf(b, j))
+
+
+        def quantize(name, b):
+            nc.vector.quantize_mx(out=codes(name, b).bitcast(FORMAT[name]), scales=scales(name, b),
+                                  in_=staged(name, b))
+
+        def quantize_part(name, b, j0, j1):
+            cols = slice(j0 * P, j1 * P)
+            nc.vector.quantize_mx(out=codes(name, b)[:, cols].bitcast(FORMAT[name]), scales=scales(name, b)[:, cols],
+                                  in_=staged_part(name, b, j0, j1))
+
+        def matmul(dst, b, left, lcols, right, rcols, start, stop):
+            nc.tensor.matmul_mx(
+                out=dst,
+                lhsT=codes(left, b)[:, lcols].bitcast(FORMAT[left]), lhsT_scale=scales(left, b)[:, lcols],
+                rhs=codes(right, b)[:, rcols].bitcast(FORMAT[right]), rhs_scale=scales(right, b)[:, rcols],
+                start=start, stop=stop)
+
+        def scores(b, c):
+            for t in range(PACK):
+                matmul(a_bank(b, c)[:, t, :], b, "q", block(t), "c", block(c), True, True)
+
+        def dscores(b, t):
+            matmul(dp_bank(b, t), b, "do", block(t), "c", slice(0, N), True, True)
+
+        def grad_dv(b, j):
+            matmul(grad_bank(b, j), b, "dom", block(j), "pw", slice(0, N), True, False)
+
+        def grad_dk(b, j):
+            matmul(grad_bank(b, j), b, "qm", block(j), "ds", slice(0, N), False, True)
+
+        def leave_psum(b, j):
+            nc.scalar.activation(out=grad_sbuf(b, j), in_=grad_bank(b, j), func=COPY)
+
+
+        def gated_dscores(b, t):
+            nc.scalar.activation(out=by_t("gated_dp%d" % b)[:, t, :], in_=dp_bank(b, t), func=COPY,
+                                 scale=gate2[:, b, t:t + 1])
+
+        def relu_times(dst, factor, b, c):
             nc.vector.scalar_tensor_tensor(
                 out=staged(dst, b)[:, chunk(c)].rearrange("p (n t) -> p n t", t=PACK),
                 in0=a_bank(b, c).rearrange("p t n -> p n t"), scalar=0.0,
-                in1=by_t(other, b)[:, :, block(c)].rearrange("p t n -> p n t"),
+                in1=by_t(factor)[:, :, block(c)].rearrange("p t n -> p n t"),
                 op0=MAX, op1=MULT)
 
-        def relu(e, b, c):
-            nc.scalar.activation(out=wide("ra", b)[:, chunk(c)].rearrange("p (n t) -> p n t", t=PACK),
-                                 in_=a_bank(b, c).rearrange("p t n -> p n t"), func=RELU)
+        def make_ds(b, c):
+            relu_times("ds", "gated_dp%d" % b, b, c)
 
-        def square(e, b, c):
-            nc.scalar.activation(out=wide("ga", b)[:, chunk(c)], in_=wide("ra", b)[:, chunk(c)], func=SQUARE)
+        def make_pw0(c):
+            for t in range(PACK):
+                nc.scalar.activation(out=by_t("gated_a")[:, t, block(c)], in_=a_bank(0, c)[:, t, :], func=COPY,
+                                     scale=gate[:, 0, t:t + 1])
+            relu_times("pw", "gated_a", 0, c)
 
-        def times_gate(e, b, k):
-            cols = slice(k * 2 * P, (k + 1) * 2 * P)
-            (nc.vector if e == "v" else nc.gpsimd).tensor_tensor(
-                out=staged("pw", b)[:, cols].rearrange("p (n t) -> p n t", t=PACK),
-                in0=wide("ga", b)[:, cols].rearrange("p (n t) -> p n t", t=PACK),
-                in1=gate[:, b, :].unsqueeze(1).to_broadcast([P, 2 * P // PACK, PACK]),
+
+        def relu1(c):
+            nc.scalar.activation(out=wide("relu_a")[:, chunk(c)].rearrange("p (n t) -> p n t", t=PACK),
+                                 in_=a_bank(1, c).rearrange("p t n -> p n t"), func=RELU)
+
+        def square1(c):
+            nc.scalar.activation(out=wide("squares")[:, chunk(c)], in_=wide("relu_a")[:, chunk(c)], func=SQUARE)
+
+        def times_gate1(engine, k):
+            cols = slice(k * GATE_STEP, (k + 1) * GATE_STEP)
+            (nc.vector if engine == VECTOR else nc.gpsimd).tensor_tensor(
+                out=staged("pw", 1)[:, cols].rearrange("p (n t) -> p n t", t=PACK),
+                in0=wide("squares")[:, cols].rearrange("p (n t) -> p n t", t=PACK),
+                in1=gate[:, 1, :].unsqueeze(1).to_broadcast([P, GATE_STEP // PACK, PACK]),
                 op=MULT)
 
-        def relu_product(e, b, k):
-            cols = slice(k * 2 * P, (k + 1) * 2 * P)
-            (nc.vector if e == "v" else nc.gpsimd).tensor_tensor(
-                out=staged("ds", b)[:, cols].rearrange("p (n t) -> p n t", t=PACK),
-                in0=wide("ra", b)[:, cols].rearrange("p (n t) -> p n t", t=PACK),
-                in1=by_t("gdp", b)[:, :, k * P // 2:(k + 1) * P // 2].rearrange("p t n -> p n t"),
-                op=MULT)
+        def make_pw1(c):
+            relu1(c)
+            square1(c)
+            times_gate1(GPSIMD, 2 * c)
+            times_gate1(GPSIMD, 2 * c + 1)
 
-        def grad_dv(e, b, j):
-            matmul(grad_bank(b, j), b, "dom", block(j), "pw", slice(0, N), True, False)
+        def gradient(b, j):
+            grad_dv(b, j)
+            grad_dk(b, j)
+            leave_psum(b, j)
 
-        def grad_dk(e, b, j):
-            matmul(grad_bank(b, j), b, "qm", block(j), "ds", slice(0, N), False, True)
 
-        def result(b, j):
-            return tile("res%d%d" % (b, j), [P, N], F32)
-
-        def leave(e, b, j):
-            cast(e, result(b, j), grad_bank(b, j))
-
-        def scatter(e, b, j):
-            nc.vector.tensor_copy(out=window(j).indirect(listed(b)), in_=result(b, j))
-
-        def store(e, j):
-            nc.sync.dma_start(out=out[block(j), :], in_=window(j))
-
-        def step(engines, fn, label, *args):
-            steps[label + "".join(str(a) for a in args)] = (engines, fn, args)
-
-        step("-", load_gate, "gate")
-        step("-", load_pool, "Lc", 0, 0)
-        step("-", load_list, "list")
-        step("-", load_pool, "Lc", 0, 1)
-        step("-", load_pool, "Lc", 1, 0)
-        step("-", load_pool, "Lc", 1, 1)
-        for name in ("q", "do", "dom", "qm"):
-            step("-", load, "L", name, 0)
-        for j in range(4):
-            step("vg" if j < 2 else "gv", zero, "zero", j)
+        load_pool(0, 0)
+        load_list()
+        load_pool(0, 1)
+        load_pool(1, 1)
         for h in range(2):
-            for c0 in (0, 512):
-                step("sv" if h == 0 else "vs", cast_pool, "P", 0, h, c0, c0 + 512)
-        step("-", gather, "G", 0, 0)
-        step("-", gather, "G", 1, 0)
-        for c0 in (0, 512):
-            step("sv", cast_pool, "P", 1, 0, c0, c0 + 512)
-        for c0 in (0, 256, 512, 768):
-            step("vs" if c0 < 512 else "sv", cast_pool, "P", 1, 1, c0, c0 + 256)
-        for name in ("q", "do", "dom", "qm"):
-            step("-", load, "L", name, 1)
-        for b in range(B):
-            step("-", gather, "G", b, 1)
-            if PLAIN[b]:
-                step("vsg", weave, "W", b)
-            step("-", quant, "Q", "c", b)
-            for name in ("q", "do"):
-                for k in range(4):
-                    step("svg", cast_turned, "T", name, b, k)
-                step("-", quant, "Q", name, b)
-            for c in range(4):
-                step("-", scores, "A", b, c)
-            for t in range(PACK):
-                step("-", dscores, "D", b, t)
-            for c in range(4):
-                if SQ[b]:
-                    step("-", relu, "R", b, c)
-                    step("-", square, "S", b, c)
-                    step("gv", times_gate, "M", b, 2 * c)
-                    step("gv", times_gate, "M", b, 2 * c + 1)
-                else:
-                    step("-", gated_a, "X", b, c)
-                    step("-", relu_times, "E", "pw", "ga", b, c)
-            for t in range(PACK):
-                step("sv", gated_dp, "Y", b, t)
-            step("-", quant, "Q", "pw", b)
-            for c in range(4):
-                if c in DSG[b]:
-                    step("gv", relu_product, "N", b, 2 * c)
-                    step("gv", relu_product, "N", b, 2 * c + 1)
-                else:
-                    step("-", relu_times, "E", "ds", "gdp", b, c)
-            step("-", quant, "Q", "ds", b)
-            for j0, j1 in GROUPS[b]:
-                for name in ("dom", "qm"):
-                    for j in range(j0, j1):
-                        step("svg", cast_plain, "C", name, b, j0, j1, j)
-                    step("-", quant_part, "Q", name, b, j0, j1)
-                for j in range(j0, j1):
-                    step("-", grad_dv, "V", b, j)
-                    step("-", grad_dk, "K", b, j)
-                    step("sv", leave, "O", b, j)
-                    step("-", scatter, "Z", b, j)
-        for j in range(4):
-            step("-", store, "St", j)
+            cast_pool(VECTOR, 0, h, 0, 512)
+            cast_pool(SCALAR, 0, h, 512, 1024)
+        gather_woven(0)
+        gather_half(0)
+        load_pool(1, 0)
+        load("q", 0)
+        load("do", 0)
+        cast_pool(SCALAR, 1, 0, 0, 512)
+        cast_pool(VECTOR, 1, 0, 512, 1024)
+        for quarter, engine in enumerate((SCALAR, SCALAR, VECTOR, SCALAR)):
+            cast_pool(engine, 1, 1, 256 * quarter, 256 * (quarter + 1))
+        load_gate()
+        load("dom", 0)
+        gather_woven(1)
+        quantize("c", 0)
 
-        for label in ORDER or list(steps):
-            engines, fn, args = steps[label]
-            fn(ENG.get(label, engines[0]), *args)
+        for quarter, engine in enumerate((SCALAR, GPSIMD, SCALAR, SCALAR)):
+            cast_turned(engine, "q", 0, quarter)
+        quantize("q", 0)
+        for quarter, engine in enumerate((SCALAR, SCALAR, VECTOR, VECTOR)):
+            cast_turned(engine, "do", 0, quarter)
+        quantize("do", 0)
+        load("q", 1)
+        scores(0, 2)
+        scores(0, 3)
+        dscores(0, 0)
+        dscores(0, 1)
+        make_pw0(2)
+        make_pw0(3)
+        load("qm", 0)
+        for j, engine in enumerate((VECTOR, VECTOR, VECTOR, GPSIMD)):
+            zero(engine, j)
+        scores(0, 0)
+        scores(0, 1)
+        make_pw0(1)
+        load("do", 1)
+        load("dom", 1)
+        dscores(0, 3)
+        make_pw0(0)
+
+        cast_plain(GPSIMD, "dom", 0, 2, 4, 2)
+        cast_plain(SCALAR, "dom", 0, 2, 4, 3)
+        quantize_part("dom", 0, 2, 4)
+        gated_dscores(0, 1)
+        cast_plain(GPSIMD, "dom", 0, 0, 2, 0)
+        cast_plain(SCALAR, "dom", 0, 0, 2, 1)
+        quantize_part("dom", 0, 0, 2)
+        cast_plain(SCALAR, "qm", 0, 0, 2, 0)
+        cast_plain(SCALAR, "qm", 0, 0, 2, 1)
+        gated_dscores(0, 0)
+        cast_turned(SCALAR, "do", 1, 0)
+        cast_turned(GPSIMD, "do", 1, 1)
+        dscores(0, 2)
+        gated_dscores(0, 2)
+        gated_dscores(0, 3)
+        quantize("pw", 0)
+        for c in range(4):
+            make_ds(0, c)
+        quantize("ds", 0)
+
+        gather_half(1)
+        weave_halves()
+        cast_turned(SCALAR, "do", 1, 3)
+        cast_turned(SCALAR, "q", 1, 1)
+        cast_turned(SCALAR, "q", 1, 2)
+        cast_turned(VECTOR, "q", 1, 3)
+        cast_plain(GPSIMD, "qm", 0, 2, 4, 2)
+        cast_plain(GPSIMD, "qm", 0, 2, 4, 3)
+        quantize_part("qm", 0, 2, 4)
+        grad_dv(0, 2)
+        cast_turned(SCALAR, "do", 1, 2)
+        grad_dv(0, 3)
+        grad_dk(0, 3)
+        quantize("c", 1)
+        cast_turned(GPSIMD, "q", 1, 0)
+        quantize_part("qm", 0, 0, 2)
+        grad_dv(0, 0)
+        quantize("q", 1)
+        gradient(0, 1)
+        scatter(0, 1)
+        quantize("do", 1)
+        dscores(1, 0)
+        dscores(1, 1)
+        leave_psum(0, 3)
+        scatter(0, 3)
+        grad_dk(0, 0)
+        leave_psum(0, 0)
+        scatter(0, 0)
+
+        load("qm", 1)
+        dscores(1, 3)
+        gated_dscores(1, 0)
+        for c in (2, 3, 0, 1):
+            scores(1, c)
+        gated_dscores(1, 3)
+        dscores(1, 2)
+        make_pw1(2)
+        make_pw1(0)
+        relu1(1)
+        gated_dscores(1, 1)
+        gated_dscores(1, 2)
+        make_pw1(3)
+        for c in range(4):
+            make_ds(1, c)
+        square1(1)
+        for j, engine in enumerate((GPSIMD, SCALAR, SCALAR, SCALAR)):
+            cast_plain(engine, "dom", 1, 0, 4, j)
+        quantize_part("dom", 1, 0, 4)
+        for j in range(4):
+            cast_plain(SCALAR, "qm", 1, 0, 4, j)
+        times_gate1(GPSIMD, 2)
+        times_gate1(VECTOR, 3)
+        quantize("pw", 1)
+        quantize("ds", 1)
+        quantize_part("qm", 1, 0, 4)
+
+        gradient(1, 3)
+        gradient(1, 2)
+        grad_dk(0, 2)
+        leave_psum(0, 2)
+        scatter(0, 2)
+        gradient(1, 0)
+        gradient(1, 1)
+        for j in (3, 2, 1, 0):
+            scatter(1, j)
+            store(j)

from contextlib import ExitStack

import concourse.mybir as mybir

B, N, T, D, R = 2, 512, 2048, 512, 512
FLOPS = 4 * 2 * B * N * D * R

F32 = mybir.dt.float32
BF16 = mybir.dt.bfloat16
U32 = mybir.dt.uint32
U16 = mybir.dt.uint16
U8 = mybir.dt.uint8
E4M3 = mybir.dt.float8_e4m3fn_x4
E5M2 = mybir.dt.float8_e5m2_x4
RELU = mybir.ActivationFunctionType.Relu
SQUARE = mybir.ActivationFunctionType.Square
COPY = mybir.ActivationFunctionType.Copy
MULT = mybir.AluOpType.mult
ADD = mybir.AluOpType.add
MAX = mybir.AluOpType.max

VECTOR, SCALAR, GPSIMD = "vector", "scalar", "gpsimd"

P = 128
PACK = 4
WIDTH = 512
LIST_COLS = N // 16
HALF = T // 2
LINE = 4
TURN = 32
GATE_STEP = 256
FORMAT = {"c": E4M3, "q": E4M3, "do": E5M2, "qm": E4M3, "dom": E5M2, "pw": E4M3, "ds": E5M2}

SBUF_TURNS = [
    ["raw_c00", "bf_q0"],
    ["raw_c01", "halves"],
    ["raw_c10", "gated_dp0"],
    ["pairs1", "bf_c1"],
    ["raw_q0", "raw_dom1"],
    ["raw_do0", "bf_dom0_2"],
    ["raw_q1", "codes_do1"],
    ["bf_do0", "raw_do1", "relu_a", "bf_qm1_0"],
    ["bf_dom0_0", "bf_qm0_2"],
    ["bf_dom1_0", "codes_ds1"],
    ["codes_dom0", "grad_sb03"],
    ["codes_c1", "codes_dom1"],
    ["codes_pw0", "raw_qm1"],
    ["squares", "codes_qm1"],
]
PSUM_TURNS = [
    ["dp00", "dp10", "a11", "grad13", "grad11"],
    ["dp01", "dp02", "a12"],
    ["dp03", "a10"],
    ["a00", "grad03", "dp13", "dp12"],
    ["a01", "a13"],
    ["a02", "grad01", "dp11", "grad12", "grad10"],
    ["a03", "grad02"],
]
BUFFER = {name: turns[0] for turns in SBUF_TURNS + PSUM_TURNS for name in turns}


def tile_attend_gat_c_kernel(tc, qT, cT, doT, rw, qm, dom, offs, out):
    nc = tc.nc
    source = {"q": qT, "do": doT, "qm": qm, "dom": dom}

    with ExitStack() as ctx:
        keep = ctx.enter_context(tc.tile_pool(name="keep", bufs=1))
        work = ctx.enter_context(tc.tile_pool(name="work", bufs=1))
        psum = ctx.enter_context(tc.psum_pool(name="psum", bufs=1))
        tiles = {}


        def tile(name, shape, dtype):
            if name not in tiles:
                tiles[name] = work.tile(shape, dtype, name=name, tag=BUFFER.get(name, name), align_bytes=64)
            return tiles[name][:]

        def bank(name, shape):
            if name not in tiles:
                tiles[name] = psum.tile(shape, F32, name=name, tag=BUFFER.get(name, name))
            return tiles[name][:]

        gate = keep.tile([P, B, PACK], F32, name="gate")
        gate2 = keep.tile([P, B, PACK], F32, name="gate2")
        offsets = keep.tile([P, B * LIST_COLS], U16, name="offsets")

        def listed(b):
            return offsets[:, b * LIST_COLS:(b + 1) * LIST_COLS]

        def block(i):
            return slice(i * P, (i + 1) * P)

        def raw_pool(u, h):
            return tile("raw_c%d%d" % (u, h), [P, 2, HALF], F32)

        def pairs(u):
            return tile("pairs%d" % u, [P, 2 * T], BF16)

        def halves():
            return tile("halves", [P, 6 * N], BF16)

        def raw(name, b):
            return tile("raw_%s%d" % (name, b), [P, PACK, WIDTH], F32)

        def staged(name, b):
            if (name, b) == ("pw", 0):
                return halves()[:, 2 * N:6 * N]
            return tile("bf_%s%d" % (name, b), [P, PACK * WIDTH], BF16)

        def staged_part(name, b, j0, j1):
            return tile("bf_%s%d_%d" % (name, b, j0), [P, PACK * P * (j1 - j0)], BF16)

        def codes(name, b):
            return tile("codes_%s%d" % (name, b), [P, WIDTH], U32)

        def scales(name, b):
            return tile("scales_%s%d" % (name, b), [P, WIDTH], U8)

        def a_bank(b, c):
            return bank("a%d%d" % (b, c), [P, PACK, P])

        def dp_bank(b, t):
            return bank("dp%d%d" % (b, t), [P, N])

        def grad_bank(b, j):
            return bank("grad%d%d" % (b, j), [P, N])

        def wide(name):
            return tile(name, [P, PACK * N], F32)

        def by_t(name):
            return wide(name).rearrange("p (t n) -> p t n", t=PACK)

        def chunk(c):
            return slice(c * PACK * P, (c + 1) * PACK * P)

        def grad_sbuf(b, j):
            return tile("grad_sb%d%d" % (b, j), [P, N], F32)

        def window(j):
            return tile("window%d" % j, [P, T], F32)


        def load_gate():
            nc.sync.dma_start(out=gate[:], in_=rw.rearrange("b (p j) o -> p b (j o)", j=PACK))
            nc.scalar.activation(out=gate2[:], in_=gate[:], func=COPY, scale=2.0)

        def load_list():
            nc.sync.dma_start(offsets[:], offs)

        def load_pool(u, h):
            view = cT.rearrange("(p j) t -> p j t", j=PACK)
            nc.sync.dma_start(out=raw_pool(u, h), in_=view[:, 2 * u:2 * u + 2, h * HALF:(h + 1) * HALF])

        def load(name, b):
            nc.sync.dma_start(out=raw(name, b), in_=source[name][b].rearrange("(p j) w -> p j w", j=PACK))

        def store(j):
            nc.sync.dma_start(out=out[block(j), :], in_=window(j))


        def cast(engine, dst, src):
            if engine == VECTOR:
                nc.vector.tensor_copy(out=dst, in_=src)
            elif engine == SCALAR:
                nc.scalar.activation(out=dst, in_=src, func=COPY)
            else:
                nc.gpsimd.tensor_scalar(out=dst, in0=src, scalar1=1.0, scalar2=0.0, op0=MULT, op1=ADD)

        def cast_pool(engine, u, h, c0, c1):
            first = h * HALF
            dst = pairs(u)[:, 2 * (first + c0):2 * (first + c1)].rearrange("p (c i e) -> p c e i", i=LINE, e=2)
            cast(engine, dst, raw_pool(u, h)[:, :, c0:c1].rearrange("p e (c i) -> p c e i", i=LINE))

        def cast_turned(engine, name, b, quarter):
            ms = slice(TURN * quarter, TURN * (quarter + 1))
            cast(engine, staged(name, b).rearrange("p (t m j) -> p m t j", t=PACK, j=PACK)[:, ms],
                 raw(name, b).rearrange("p j (m t) -> p m t j", t=PACK)[:, ms])

        def cast_plain(engine, name, b, j0, j1, j):
            dst = staged_part(name, b, j0, j1)[:, PACK * P * (j - j0):PACK * P * (j + 1 - j0)]
            cast(engine, dst.rearrange("p (c i j) -> p c j i", i=LINE, j=PACK),
                 raw(name, b)[:, :, block(j)].rearrange("p j (c i) -> p c j i", i=LINE))


        def gather(b, u, dst):
            nc.vector.tensor_copy(out=dst, in_=pairs(u).bitcast(U32).indirect(listed(b)))

        def gather_woven(u):
            gather(0, u, staged("c", 0).bitcast(U32)[:, u:2 * N:2])

        def gather_half(u):
            gather(1, u, halves()[:, 2 * u * N:2 * (u + 1) * N].bitcast(U32))

        def weave_halves():
            nc.scalar.copy(out=staged("c", 1).rearrange("p (n u e) -> p n u e", u=2, e=2),
                           in_=halves()[:, 0:4 * N].rearrange("p (u n e) -> p n u e", u=2, e=2))

        def zero(engine, j):
            (nc.vector if engine == VECTOR else nc.gpsimd).memset(window(j), 0.0)

        def scatter(b, j):
            nc.vector.tensor_copy(out=window(j).indirect(listed(b)), in_=grad_sbuf(b, j))


        def quantize(name, b):
            nc.vector.quantize_mx(out=codes(name, b).bitcast(FORMAT[name]), scales=scales(name, b),
                                  in_=staged(name, b))

        def quantize_part(name, b, j0, j1):
            cols = slice(j0 * P, j1 * P)
            nc.vector.quantize_mx(out=codes(name, b)[:, cols].bitcast(FORMAT[name]), scales=scales(name, b)[:, cols],
                                  in_=staged_part(name, b, j0, j1))

        def matmul(dst, b, left, lcols, right, rcols, start, stop):
            nc.tensor.matmul_mx(
                out=dst,
                lhsT=codes(left, b)[:, lcols].bitcast(FORMAT[left]), lhsT_scale=scales(left, b)[:, lcols],
                rhs=codes(right, b)[:, rcols].bitcast(FORMAT[right]), rhs_scale=scales(right, b)[:, rcols],
                start=start, stop=stop)

        def scores(b, c):
            for t in range(PACK):
                matmul(a_bank(b, c)[:, t, :], b, "q", block(t), "c", block(c), True, True)

        def dscores(b, t):
            matmul(dp_bank(b, t), b, "do", block(t), "c", slice(0, N), True, True)

        def grad_dv(b, j):
            matmul(grad_bank(b, j), b, "dom", block(j), "pw", slice(0, N), True, False)

        def grad_dk(b, j):
            matmul(grad_bank(b, j), b, "qm", block(j), "ds", slice(0, N), False, True)

        def leave_psum(b, j):
            nc.scalar.activation(out=grad_sbuf(b, j), in_=grad_bank(b, j), func=COPY)


        def gated_dscores(b, t):
            nc.scalar.activation(out=by_t("gated_dp%d" % b)[:, t, :], in_=dp_bank(b, t), func=COPY,
                                 scale=gate2[:, b, t:t + 1])

        def relu_times(dst, factor, b, c):
            nc.vector.scalar_tensor_tensor(
                out=staged(dst, b)[:, chunk(c)].rearrange("p (n t) -> p n t", t=PACK),
                in0=a_bank(b, c).rearrange("p t n -> p n t"), scalar=0.0,
                in1=by_t(factor)[:, :, block(c)].rearrange("p t n -> p n t"),
                op0=MAX, op1=MULT)

        def make_ds(b, c):
            relu_times("ds", "gated_dp%d" % b, b, c)

        def make_pw0(c):
            for t in range(PACK):
                nc.scalar.activation(out=by_t("gated_a")[:, t, block(c)], in_=a_bank(0, c)[:, t, :], func=COPY,
                                     scale=gate[:, 0, t:t + 1])
            relu_times("pw", "gated_a", 0, c)


        def relu1(c):
            nc.scalar.activation(out=wide("relu_a")[:, chunk(c)].rearrange("p (n t) -> p n t", t=PACK),
                                 in_=a_bank(1, c).rearrange("p t n -> p n t"), func=RELU)

        def square1(c):
            nc.scalar.activation(out=wide("squares")[:, chunk(c)], in_=wide("relu_a")[:, chunk(c)], func=SQUARE)

        def times_gate1(engine, k):
            cols = slice(k * GATE_STEP, (k + 1) * GATE_STEP)
            (nc.vector if engine == VECTOR else nc.gpsimd).tensor_tensor(
                out=staged("pw", 1)[:, cols].rearrange("p (n t) -> p n t", t=PACK),
                in0=wide("squares")[:, cols].rearrange("p (n t) -> p n t", t=PACK),
                in1=gate[:, 1, :].unsqueeze(1).to_broadcast([P, GATE_STEP // PACK, PACK]),
                op=MULT)

        def make_pw1(c):
            relu1(c)
            square1(c)
            times_gate1(GPSIMD, 2 * c)
            times_gate1(GPSIMD, 2 * c + 1)

        def gradient(b, j):
            grad_dv(b, j)
            grad_dk(b, j)
            leave_psum(b, j)


        load_pool(0, 0)
        load_list()
        load_pool(0, 1)
        load_pool(1, 1)
        for h in range(2):
            cast_pool(VECTOR, 0, h, 0, 512)
            cast_pool(SCALAR, 0, h, 512, 1024)
        gather_woven(0)
        gather_half(0)
        load_pool(1, 0)
        load("q", 0)
        load("do", 0)
        cast_pool(SCALAR, 1, 0, 0, 512)
        cast_pool(VECTOR, 1, 0, 512, 1024)
        for quarter, engine in enumerate((SCALAR, SCALAR, VECTOR, SCALAR)):
            cast_pool(engine, 1, 1, 256 * quarter, 256 * (quarter + 1))
        load_gate()
        load("dom", 0)
        gather_woven(1)
        quantize("c", 0)

        for quarter, engine in enumerate((SCALAR, GPSIMD, SCALAR, SCALAR)):
            cast_turned(engine, "q", 0, quarter)
        quantize("q", 0)
        for quarter, engine in enumerate((SCALAR, SCALAR, VECTOR, VECTOR)):
            cast_turned(engine, "do", 0, quarter)
        quantize("do", 0)
        load("q", 1)
        scores(0, 2)
        scores(0, 3)
        dscores(0, 0)
        dscores(0, 1)
        make_pw0(2)
        make_pw0(3)
        load("qm", 0)
        for j, engine in enumerate((VECTOR, VECTOR, VECTOR, GPSIMD)):
            zero(engine, j)
        scores(0, 0)
        scores(0, 1)
        make_pw0(1)
        load("do", 1)
        load("dom", 1)
        dscores(0, 3)
        make_pw0(0)

        cast_plain(GPSIMD, "dom", 0, 2, 4, 2)
        cast_plain(SCALAR, "dom", 0, 2, 4, 3)
        quantize_part("dom", 0, 2, 4)
        gated_dscores(0, 1)
        cast_plain(GPSIMD, "dom", 0, 0, 2, 0)
        cast_plain(SCALAR, "dom", 0, 0, 2, 1)
        quantize_part("dom", 0, 0, 2)
        cast_plain(SCALAR, "qm", 0, 0, 2, 0)
        cast_plain(SCALAR, "qm", 0, 0, 2, 1)
        gated_dscores(0, 0)
        cast_turned(SCALAR, "do", 1, 0)
        cast_turned(GPSIMD, "do", 1, 1)
        dscores(0, 2)
        gated_dscores(0, 2)
        gated_dscores(0, 3)
        quantize("pw", 0)
        for c in range(4):
            make_ds(0, c)
        quantize("ds", 0)

        gather_half(1)
        weave_halves()
        cast_turned(SCALAR, "do", 1, 3)
        cast_turned(SCALAR, "q", 1, 1)
        cast_turned(SCALAR, "q", 1, 2)
        cast_turned(VECTOR, "q", 1, 3)
        cast_plain(GPSIMD, "qm", 0, 2, 4, 2)
        cast_plain(GPSIMD, "qm", 0, 2, 4, 3)
        quantize_part("qm", 0, 2, 4)
        grad_dv(0, 2)
        cast_turned(SCALAR, "do", 1, 2)
        grad_dv(0, 3)
        grad_dk(0, 3)
        quantize("c", 1)
        cast_turned(GPSIMD, "q", 1, 0)
        quantize_part("qm", 0, 0, 2)
        grad_dv(0, 0)
        quantize("q", 1)
        gradient(0, 1)
        scatter(0, 1)
        quantize("do", 1)
        dscores(1, 0)
        dscores(1, 1)
        leave_psum(0, 3)
        scatter(0, 3)
        grad_dk(0, 0)
        leave_psum(0, 0)
        scatter(0, 0)

        load("qm", 1)
        dscores(1, 3)
        gated_dscores(1, 0)
        for c in (2, 3, 0, 1):
            scores(1, c)
        gated_dscores(1, 3)
        dscores(1, 2)
        make_pw1(2)
        make_pw1(0)
        relu1(1)
        gated_dscores(1, 1)
        gated_dscores(1, 2)
        make_pw1(3)
        for c in range(4):
            make_ds(1, c)
        square1(1)
        for j, engine in enumerate((GPSIMD, SCALAR, SCALAR, SCALAR)):
            cast_plain(engine, "dom", 1, 0, 4, j)
        quantize_part("dom", 1, 0, 4)
        for j in range(4):
            cast_plain(SCALAR, "qm", 1, 0, 4, j)
        times_gate1(GPSIMD, 2)
        times_gate1(VECTOR, 3)
        quantize("pw", 1)
        quantize("ds", 1)
        quantize_part("qm", 1, 0, 4)

        gradient(1, 3)
        gradient(1, 2)
        grad_dk(0, 2)
        leave_psum(0, 2)
        scatter(0, 2)
        gradient(1, 0)
        gradient(1, 1)
        for j in (3, 2, 1, 0):
            scatter(1, j)
            store(j)
